import numpy as np
import ml_dtypes


def mxq(x, axis, fmt="e4m3"):
    dtype, down = {"e4m3": (ml_dtypes.float8_e4m3fn, 7), "e5m2": (ml_dtypes.float8_e5m2, 14)}[fmt]
    v = np.moveaxis(np.asarray(x, np.float32).astype(ml_dtypes.bfloat16).astype(np.float64), axis, -1)
    blocks = v.reshape(v.shape[:-1] + (-1, 32))
    amax = np.abs(blocks).max(-1, keepdims=True)
    byte = np.maximum(np.where(amax > 0, np.frexp(amax)[1] - 1 + 127, 0) - down, 1)
    scale = np.exp2(byte - 127.0)
    codes = (blocks / scale).astype(np.float32).astype(dtype).astype(np.float64)
    return np.moveaxis((codes * scale).reshape(v.shape), -1, axis)


WIDE = False


def mx_kscale(k):
    if not WIDE:
        return np.ones(k)
    levels = np.array([10, -10, 5, -5, 0])
    if k % 512:
        return np.exp2(np.random.permutation(np.resize(levels, k // 32))).repeat(32)
    a = np.empty((k // 512, 16))
    for p in range(k // 512):
        a[p, :8] = np.random.permutation(np.resize(levels, 8))
        for g in range(8):
            far = levels[np.abs(levels - a[p, g]) >= 10]
            a[p, g + 8] = far[np.random.randint(len(far))]
    return np.exp2(a.ravel()).repeat(32)


def f64(x):
    return np.asarray(x).astype(np.float64)


def striped(idx):
    return np.tile(idx.reshape(-1, 16).T, (8, 1)).astype(np.uint16)


def unstriped(offs):
    return offs[:16].T.reshape(-1).astype(np.int64)


def pack_weight(w):
    k, n = w.shape
    w = f64(np.asarray(w, np.float32).astype(ml_dtypes.bfloat16)).reshape(k // 32, 32, n)
    amax = np.abs(w).max(1)
    byte = np.clip(np.where(amax > 0, np.frexp(amax)[1] - 1 + 127 - 7, 1), 1, 254)
    scaled = (w * np.exp2(127.0 - byte)[:, None, :]).reshape(k, n).astype(np.float32)
    words = np.ascontiguousarray(scaled.reshape(k // 512, 128, 4, n).transpose(0, 1, 3, 2)).astype(ml_dtypes.float8_e4m3fn).view(np.uint8)
    return words, np.ascontiguousarray(byte.astype(np.uint8).reshape(k // 512, 16, n))


def unpack_weight(words, scales):
    g, p, n, _ = words.shape
    vals = np.ascontiguousarray(words).view(ml_dtypes.float8_e4m3fn).astype(np.float64) * np.repeat(np.exp2(scales.astype(np.float64) - 127.0), 8, axis=1)[..., None]
    return vals.transpose(0, 1, 3, 2).reshape(g * 512, n)


E2M1 = np.array([0.0, 0.5, 1.0, 1.5, 2.0, 3.0, 4.0, 6.0, -0.0, -0.5, -1.0, -1.5, -2.0, -3.0, -4.0, -6.0])


def pack_fp4(w):
    k, n = w.shape
    w = f64(np.asarray(w, np.float32).astype(ml_dtypes.bfloat16)).reshape(k // 32, 32, n)
    amax = np.abs(w).max(1)
    mant, ex = np.frexp(amax / 6.0)
    byte = np.clip(np.where(amax > 0, np.where(mant > 0.5, ex, ex - 1) + 127, 1), 1, 254)
    scaled = (w * np.exp2(127.0 - byte)[:, None, :]).reshape(k, n).astype(np.float32)
    c = np.ascontiguousarray(scaled.reshape(k // 512, 128, 4, n).transpose(0, 1, 3, 2)).astype(ml_dtypes.float4_e2m1fn).view(np.uint8) & 0xF
    words = (c[..., 0::2] | (c[..., 1::2] << 4)).reshape(k // 512, 128, 2 * n)
    return np.ascontiguousarray(words), np.ascontiguousarray(byte.astype(np.uint8).reshape(k // 512, 16, n))


def unpack_fp4(words, scales):
    g, _, n = scales.shape
    words = np.ascontiguousarray(words).reshape(g, 128, n, 2)
    nib = np.empty((g, 128, n, 4), np.uint8)
    nib[..., 0::2] = words & 0xF
    nib[..., 1::2] = words >> 4
    vals = E2M1[nib] * np.repeat(np.exp2(scales.astype(np.float64) - 127.0), 8, axis=1)[..., None]
    return vals.transpose(0, 1, 3, 2).reshape(g * 512, n)


def relu(v):
    return np.maximum(v, 0.0)


def sigmoid(v):
    return 1.0 / (1.0 + np.exp(-np.maximum(v, -700.0)))


K, T, S, D, N, H = 512, 4096, 1024, 4, 256, 512


def setup_inputs():
    n = np.random.standard_normal
    s = mx_kscale(K)[:, None]
    u = mx_kscale(H)
    packed_xT = pack_weight(n((K, T)) * s)
    packed_w1 = pack_fp4(n((K, H)) / np.sqrt(K) / s)
    packed_w2 = pack_fp4(n((K, H)) / np.sqrt(K) / s)
    packed_w3 = pack_fp4(n((H, N)) / np.sqrt(H) / u[:, None])
    return {
        "x_words": packed_xT[0],
        "x_scales": packed_xT[1],
        "w1_words": packed_w1[0],
        "w1_scales": packed_w1[1],
        "w2_words": packed_w2[0],
        "w2_scales": packed_w2[1],
        "den": (np.random.uniform(2.5, 3.5, (H, S))).astype(np.float32),
        "unit": (np.random.uniform(0.6, 1.4, (H, 1)) * u[:, None]).astype(np.float32),
        "w3_words": packed_w3[0],
        "w3_scales": packed_w3[1],
        "offs": striped(np.random.permutation(T)[:S]),
        "shuf": striped(np.random.permutation(S)),
    }


def reference(x_words, x_scales, w1_words, w1_scales, w2_words, w2_scales, den, unit, w3_words, w3_scales, offs, shuf):
    xq = unpack_weight(x_words, x_scales)[:, unstriped(offs)]
    y = unpack_fp4(w1_words, w1_scales).T @ xq
    rew = sigmoid(y)
    rs = rew.reshape(len(rew), -1, D).sum(axis=2)
    base = (np.repeat(rs, D, axis=1) - rew) / f64(den)
    adv = rew - base
    yl = unpack_fp4(w2_words, w2_scales).T @ xq
    pgz = adv * relu(yl) - (0.15 * ((yl) ** 2))
    hid = f64(unit) * (pgz + adv[:, unstriped(shuf)])
    return unpack_fp4(w3_words, w3_scales).T @ mxq(hid, 0, "e4m3")

@@ -1,0 +1,209 @@
+from contextlib import ExitStack
+
+import concourse.mybir as mybir
+
+K, T, S, D, N, H = 512, 4096, 1024, 4, 256, 512
+FLOPS = 2 * S * (2 * K * H + H * N)
+
+F32 = mybir.dt.float32
+BF16 = mybir.dt.bfloat16
+I32 = mybir.dt.int32
+U32 = mybir.dt.uint32
+U16 = mybir.dt.uint16
+U8 = mybir.dt.uint8
+FP8X4 = mybir.dt.float8_e4m3fn_x4
+FP4X4 = mybir.dt.float4_e2m1fn_x4
+ALU = mybir.AluOpType
+ACT = mybir.ActivationFunctionType
+
+P = 128
+PACK = 4
+HALF = 512
+REF = 32
+BLOCKS = ((0, 512), (512, 256), (768, 128), (896, 128))
+
+
+def load_scale_rows(queue, plane, rows):
+    for q in range(4):
+        queue.dma_start(out=plane[32 * q : 32 * q + 4, :].bitcast(I32), in_=rows[4 * q : 4 * q + 4, :].bitcast(I32))
+
+
+def tile_picked_yrloov_pen_p_kernel(
+    tc, x_words, x_scales, w1_words, w1_scales, w2_words, w2_scales, den, unit, w3_words, w3_scales, offs, shuf, out
+):
+    nc = tc.nc
+    with ExitStack() as ctx:
+        keep = ctx.enter_context(tc.tile_pool(name="keep", bufs=1))
+        work = ctx.enter_context(tc.tile_pool(name="work", bufs=2))
+        psum = ctx.enter_context(tc.psum_pool(name="psum", bufs=1))
+
+        den_rows = den.rearrange("(p t) j -> p t j", t=PACK)
+        den_sb = [keep.tile([P, S], F32, name="den%d" % t) for t in range(PACK)]
+        offs_sb = keep.tile([P, S // 16], U16, name="offs_sb")
+        shuf_sb = keep.tile([P, S // 16], U16, name="shuf_sb")
+        unit_sb = keep.tile([P, PACK], F32, name="unit_sb")
+        xw = keep.tile([P, T], U32, name="xw")
+        xs = keep.tile([P, T], U8, name="xs")
+        w1w = keep.tile([P, 2 * H], U8, name="w1w")
+        w1s = keep.tile([P, H], U8, name="w1s")
+        w2w = keep.tile([P, 2 * H], U8, name="w2w")
+        w2s = keep.tile([P, H], U8, name="w2s")
+        w3w = keep.tile([P, 2 * N], U8, name="w3w", align_bytes=64)
+        w3s = keep.tile([P, N], U8, name="w3s", align_bytes=64)
+
+        nc.vector.memset(xs[:].bitcast(I32), 0)
+        nc.gpsimd.memset(w1s[:].bitcast(I32), 0)
+        nc.vector.memset(w2s[:].bitcast(I32), 0)
+        nc.vector.memset(w3s[:].bitcast(I32), 0)
+
+        nc.sync.dma_start(out=den_sb[0][:], in_=den_rows[:, 0, :])
+        nc.sync.dma_start(offs_sb[:], offs)
+        nc.sync.dma_start(out=w1w[:].bitcast(I32), in_=w1_words[0].bitcast(I32))
+        nc.sync.dma_start(out=xw[:].bitcast(I32), in_=x_words[0].rearrange("p n t -> p (n t)").bitcast(I32))
+        load_scale_rows(nc.scalar, xs, x_scales[0])
+        load_scale_rows(nc.gpsimd, w1s, w1_scales[0])
+        nc.sync.dma_start(out=unit_sb[:], in_=unit.rearrange("(p t) o -> p (t o)", t=PACK))
+        for t in range(1, PACK):
+            nc.sync.dma_start(out=den_sb[t][:], in_=den_rows[:, t, :])
+        nc.sync.dma_start(out=w2w[:].bitcast(I32), in_=w2_words[0].bitcast(I32))
+        load_scale_rows(nc.sync, w2s, w2_scales[0])
+        nc.sync.dma_start(shuf_sb[:], shuf)
+        nc.sync.dma_start(out=w3w[:].bitcast(I32), in_=w3_words[0].bitcast(I32))
+        load_scale_rows(nc.sync, w3s, w3_scales[0])
+
+        inv_ref = keep.tile([P, PACK], F32, name="inv_ref")
+        mean_ref = keep.tile([P, PACK], F32, name="mean_ref")
+        junk = keep.tile([P, REF], F32, name="junk")
+        base_gain = keep.tile([P, PACK], F32, name="base_gain")
+        sq_gain = keep.tile([P, PACK], F32, name="sq_gain")
+        rel = [keep.tile([P, S], F32, name="rel%d" % t) for t in range(PACK)]
+
+        def row_reference(t):
+            nc.vector.tensor_scalar(junk[:], den_sb[t][:, 0:REF], 1.0 / REF, 0.0, ALU.mult, ALU.add, accum_out=mean_ref[:, t : t + 1])
+            nc.vector.reciprocal(inv_ref[:, t : t + 1], mean_ref[:, t : t + 1])
+
+        def deal(words, scales, name, tag):
+            dw = keep.tile([P, 2 * H], U8, name=name + "w", tag=tag, align_bytes=64)
+            ds = keep.tile([P, H], U8, name=name + "s", align_bytes=64)
+            nc.vector.tensor_copy(
+                out=dw[:].rearrange("p (t m b) -> p t m b", t=PACK, b=2), in_=words[:].rearrange("p (m t b) -> p t m b", t=PACK, b=2)
+            )
+            nc.vector.tensor_copy(out=ds[:].rearrange("p (t m) -> p t m", t=PACK), in_=scales[:].rearrange("p (m t) -> p t m", t=PACK))
+            return dw, ds
+
+        row_reference(0)
+        log0 = keep.tile([P, S], F32, name="log0")
+        nc.scalar.activation(log0[:], den_sb[0][:], ACT.Ln, scale=inv_ref[:, 0:1])
+        nc.scalar.activation(rel[0][:], log0[:], ACT.Exp, scale=-1.0)
+
+        w1dw, w1ds = deal(w1w, w1s, "w1d", "held")
+        xgs = keep.tile([P, S], U8, name="xgs", align_bytes=64)
+        nc.vector.tensor_copy(xgs[:], xs[:].indirect(offs_sb[:]))
+        xgw = []
+        for h in range(2):
+            g = keep.tile([P, HALF], U32, name="xgw%d" % h, align_bytes=64)
+            nc.vector.tensor_copy(g[:], xw[:].indirect(offs_sb[:, h * 32 : (h + 1) * 32]))
+            xgw.append(g)
+
+        def product(bank, dw, ds, t, h):
+            nc.tensor.matmul_mx(
+                out=bank[:],
+                lhsT=dw[:, 2 * P * t : 2 * P * (t + 1)].bitcast(FP4X4),
+                lhsT_scale=ds[:, P * t : P * (t + 1)],
+                rhs=xgw[h][:].bitcast(FP8X4),
+                rhs_scale=xgs[:, h * HALF : (h + 1) * HALF],
+                start=True,
+                stop=True,
+            )
+
+        rew = [keep.tile([P, S], F32, name="rew%d" % t) for t in range(PACK)]
+        for t in range(PACK):
+            for h in range(2):
+                bank = psum.tile([P, HALF], F32, name="y", bufs=3)
+                product(bank, w1dw, w1ds, t, h)
+                nc.scalar.activation(rew[t][:, h * HALF : (h + 1) * HALF], bank[:], ACT.Sigmoid)
+
+        w2dw, w2ds = deal(w2w, w2s, "w2d", "w2dw")
+        for t in range(1, PACK):
+            row_reference(t)
+        nc.vector.tensor_tensor(base_gain[:], inv_ref[:], unit_sb[:], ALU.mult)
+        nc.vector.tensor_scalar(sq_gain[:], unit_sb[:], -0.15, None, ALU.mult)
+
+        logs = keep.tile([P, PACK - 1, S], F32, name="logs", tag="held", align_bytes=64)
+        for t in range(1, PACK):
+            nc.scalar.activation(logs[:, t - 1, :], den_sb[t][:], ACT.Ln, scale=inv_ref[:, t : t + 1])
+        for t in range(1, PACK):
+            nc.scalar.activation(rel[t][:], logs[:, t - 1, :], ACT.Exp, scale=-1.0)
+
+        others = []
+        for t in range(PACK):
+            pair = work.tile([P, S // 2], F32, name="pair")
+            two = rew[t][:].rearrange("p (g e) -> p g e", e=2)
+            nc.vector.tensor_tensor(pair[:], two[:, :, 0], two[:, :, 1], ALU.add)
+            oth = keep.tile([P, S], F32, name="others%d" % t)
+            nc.vector.tensor_tensor(
+                oth[:].rearrange("p (v h e) -> p v h e", h=2, e=2),
+                rew[t][:].rearrange("p (v h e) -> p v h e", h=2, e=2)[:, :, :, ::-1],
+                pair[:].rearrange("p (v h) -> p v h", h=2)[:, :, ::-1].unsqueeze(3).to_broadcast([P, S // D, 2, 2]),
+                ALU.add,
+            )
+            others.append(oth)
+
+        adv = []
+        for t in range(PACK):
+            base = work.tile([P, S], F32, name="base")
+            nc.vector.scalar_tensor_tensor(base[:], others[t][:], base_gain[:, t : t + 1], rel[t][:], ALU.mult, ALU.mult)
+            a = keep.tile([P, S], F32, name="adv%d" % t)
+            nc.vector.scalar_tensor_tensor(a[:], rew[t][:], unit_sb[:, t : t + 1], base[:], ALU.mult, ALU.subtract)
+            adv.append(a)
+
+        pgz = keep.tile([P, PACK, S], F32, name="pgz")
+
+        def gradient_term(t, h):
+            cols = slice(h * HALF, (h + 1) * HALF)
+            bank = psum.tile([P, HALF], F32, name="yl", bufs=3)
+            product(bank, w2dw, w2ds, t, h)
+            sq = work.tile([P, HALF], F32, name="sq", bufs=3)
+            nc.scalar.activation(sq[:], bank[:], ACT.Square)
+            pos = work.tile([P, HALF], F32, name="pos", bufs=3)
+            nc.vector.scalar_tensor_tensor(pos[:], bank[:], 0.0, adv[t][:, cols], ALU.max, ALU.mult)
+            nc.vector.scalar_tensor_tensor(pgz[:, t, cols], sq[:], sq_gain[:, t : t + 1], pos[:], ALU.mult, ALU.add)
+
+        out_rows = out.rearrange("(a p) j -> p a j", p=P)
+
+        def finish(c0, n):
+            hid = keep.tile([P, PACK, n], F32, name="hid%d" % c0)
+            for t in range(PACK):
+                nc.vector.tensor_tensor(
+                    hid[:, t, :], adv[t][:].indirect(shuf_sb[:, c0 // 16 : (c0 + n) // 16]), pgz[:, t, c0 : c0 + n], ALU.add
+                )
+            grouped = keep.tile([P, n * PACK], BF16, name="grouped%d" % c0, align_bytes=64)
+            weave = nc.vector.tensor_copy if c0 + n == S else nc.scalar.copy
+            weave(grouped[:].rearrange("p (c i t) -> p c t i", i=4, t=PACK), hid[:].rearrange("p t (c i) -> p c t i", i=4))
+            codes = keep.tile([P, n], U32, name="codes%d" % c0, align_bytes=64)
+            scales = keep.tile([P, n], U8, name="scales%d" % c0, align_bytes=64)
+            nc.vector.quantize_mx(out=codes[:].bitcast(FP8X4), scales=scales[:], in_=grouped[:])
+            res = keep.tile([P, 2, n], F32, name="res%d" % c0)
+            per_bank = min(2, HALF // n)
+            for a in range(2):
+                if a % per_bank == 0:
+                    bank = psum.tile([P, HALF], F32, name="o", bufs=2)
+                nc.tensor.matmul_mx(
+                    out=bank[:, (a % per_bank) * n : (a % per_bank + 1) * n],
+                    lhsT=w3w[:, 2 * P * a : 2 * P * (a + 1)].bitcast(FP4X4),
+                    lhsT_scale=w3s[:, P * a : P * (a + 1)],
+                    rhs=codes[:].bitcast(FP8X4),
+                    rhs_scale=scales[:],
+                    start=True,
+                    stop=True,
+                )
+                if (a + 1) % per_bank == 0:
+                    nc.scalar.copy(res[:, a + 1 - per_bank : a + 1, :].rearrange("p a j -> p (a j)"), bank[:, 0 : per_bank * n])
+            nc.sync.dma_start(out=out_rows[:, :, c0 : c0 + n], in_=res[:])
+
+        for h in range(2):
+            for t in range(PACK):
+                gradient_term(t, h)
+            for c0, n in BLOCKS:
+                if c0 // HALF == h:
+                    finish(c0, n)

@@ -1,6 +1,7 @@
 from contextlib import ExitStack
 
 import concourse.mybir as mybir
+from concourse.masks import make_identity
 
 K, T, S, D, N, H = 512, 4096, 1024, 4, 256, 512
 FLOPS = 2 * S * (2 * K * H + H * N)
@@ -20,12 +21,16 @@ P = 128
 PACK = 4
 HALF = 512
 REF = 32
-BLOCKS = ((0, 512), (512, 256), (768, 128), (896, 128))
+DIRECT = 1
+EARLY = 2
+LATE_FETCH = 2
+TURNED_WIDTHS = (256, 128)
+BLOCKS = ((0, 256), (256, 256), (512, 256), (768, 128), (896, 128))
 
 
-def load_scale_rows(queue, plane, rows):
+def load_scale_rows(queues, plane, rows):
     for q in range(4):
-        queue.dma_start(out=plane[32 * q : 32 * q + 4, :].bitcast(I32), in_=rows[4 * q : 4 * q + 4, :].bitcast(I32))
+        queues[q].dma_start(out=plane[32 * q : 32 * q + 4, :].bitcast(I32), in_=rows[4 * q : 4 * q + 4, :].bitcast(I32))
 
 
 def tile_picked_yrloov_pen_p_kernel(
@@ -34,76 +39,95 @@ def tile_picked_yrloov_pen_p_kernel(
     nc = tc.nc
     with ExitStack() as ctx:
         keep = ctx.enter_context(tc.tile_pool(name="keep", bufs=1))
+        placed = ctx.enter_context(tc.tile_pool(name="placed", bufs=1))
         work = ctx.enter_context(tc.tile_pool(name="work", bufs=2))
         psum = ctx.enter_context(tc.psum_pool(name="psum", bufs=1))
 
         den_rows = den.rearrange("(p t) j -> p t j", t=PACK)
-        den_sb = [keep.tile([P, S], F32, name="den%d" % t) for t in range(PACK)]
         offs_sb = keep.tile([P, S // 16], U16, name="offs_sb")
         shuf_sb = keep.tile([P, S // 16], U16, name="shuf_sb")
-        unit_sb = keep.tile([P, PACK], F32, name="unit_sb")
-        xw = keep.tile([P, T], U32, name="xw")
-        xs = keep.tile([P, T], U8, name="xs")
+        den_early = placed.tile([P, EARLY, S], F32, name="den_early", offset=49152)
+        xs = placed.tile([P, T], U8, name="xs", offset=57344)
         w1w = keep.tile([P, 2 * H], U8, name="w1w")
-        w1s = keep.tile([P, H], U8, name="w1s")
-        w2w = keep.tile([P, 2 * H], U8, name="w2w")
-        w2s = keep.tile([P, H], U8, name="w2s")
-        w3w = keep.tile([P, 2 * N], U8, name="w3w", align_bytes=64)
-        w3s = keep.tile([P, N], U8, name="w3s", align_bytes=64)
+        xw = placed.tile([P, T], U32, name="xw", offset=0)
+        w1s = placed.tile([P, H], U8, name="w1s", offset=4 * T)
+        log_early = placed.tile([P, EARLY, S], F32, name="log_early", offset=20480)
 
         nc.vector.memset(xs[:].bitcast(I32), 0)
-        nc.gpsimd.memset(w1s[:].bitcast(I32), 0)
-        nc.vector.memset(w2s[:].bitcast(I32), 0)
-        nc.vector.memset(w3s[:].bitcast(I32), 0)
+        nc.vector.memset(w1s[:].bitcast(I32), 0)
 
-        nc.sync.dma_start(out=den_sb[0][:], in_=den_rows[:, 0, :])
         nc.sync.dma_start(offs_sb[:], offs)
         nc.sync.dma_start(out=w1w[:].bitcast(I32), in_=w1_words[0].bitcast(I32))
-        nc.sync.dma_start(out=xw[:].bitcast(I32), in_=x_words[0].rearrange("p n t -> p (n t)").bitcast(I32))
-        load_scale_rows(nc.scalar, xs, x_scales[0])
-        load_scale_rows(nc.gpsimd, w1s, w1_scales[0])
-        nc.sync.dma_start(out=unit_sb[:], in_=unit.rearrange("(p t) o -> p (t o)", t=PACK))
-        for t in range(1, PACK):
-            nc.sync.dma_start(out=den_sb[t][:], in_=den_rows[:, t, :])
-        nc.sync.dma_start(out=w2w[:].bitcast(I32), in_=w2_words[0].bitcast(I32))
-        load_scale_rows(nc.sync, w2s, w2_scales[0])
         nc.sync.dma_start(shuf_sb[:], shuf)
-        nc.sync.dma_start(out=w3w[:].bitcast(I32), in_=w3_words[0].bitcast(I32))
-        load_scale_rows(nc.sync, w3s, w3_scales[0])
+        for t in range(EARLY):
+            nc.scalar.dma_start(out=den_early[:, t, :], in_=den_rows[:, t, :])
+        nc.scalar.dma_start(out=xw[:].bitcast(I32), in_=x_words[0].rearrange("p n t -> p (n t)").bitcast(I32))
+        load_scale_rows([nc.sync] * 4, xs, x_scales[0])
+        load_scale_rows([nc.sync, nc.sync, nc.gpsimd, nc.gpsimd], w1s, w1_scales[0])
+        ident = keep.tile([P, P], F32, name="ident")
+        make_identity(nc, ident[:])
 
         inv_ref = keep.tile([P, PACK], F32, name="inv_ref")
         mean_ref = keep.tile([P, PACK], F32, name="mean_ref")
-        junk = keep.tile([P, REF], F32, name="junk")
         base_gain = keep.tile([P, PACK], F32, name="base_gain")
         sq_gain = keep.tile([P, PACK], F32, name="sq_gain")
         rel = [keep.tile([P, S], F32, name="rel%d" % t) for t in range(PACK)]
 
-        def row_reference(t):
-            nc.vector.tensor_scalar(junk[:], den_sb[t][:, 0:REF], 1.0 / REF, 0.0, ALU.mult, ALU.add, accum_out=mean_ref[:, t : t + 1])
+        def row_reference(t, rows, scratch):
+            nc.vector.tensor_scalar(scratch, rows[:, 0:REF], 1.0 / REF, 0.0, ALU.mult, ALU.add, accum_out=mean_ref[:, t : t + 1])
             nc.vector.reciprocal(inv_ref[:, t : t + 1], mean_ref[:, t : t + 1])
 
-        def deal(words, scales, name, tag):
-            dw = keep.tile([P, 2 * H], U8, name=name + "w", tag=tag, align_bytes=64)
-            ds = keep.tile([P, H], U8, name=name + "s", align_bytes=64)
+        def deal_words(words, dw):
             nc.vector.tensor_copy(
                 out=dw[:].rearrange("p (t m b) -> p t m b", t=PACK, b=2), in_=words[:].rearrange("p (m t b) -> p t m b", t=PACK, b=2)
             )
+
+        def deal_scales(scales, ds):
             nc.vector.tensor_copy(out=ds[:].rearrange("p (t m) -> p t m", t=PACK), in_=scales[:].rearrange("p (m t) -> p t m", t=PACK))
-            return dw, ds
 
-        row_reference(0)
-        log0 = keep.tile([P, S], F32, name="log0")
-        nc.scalar.activation(log0[:], den_sb[0][:], ACT.Ln, scale=inv_ref[:, 0:1])
-        nc.scalar.activation(rel[0][:], log0[:], ACT.Exp, scale=-1.0)
+        scratch_early = keep.tile([P, REF], F32, name="scratch_early")
+        for t in range(EARLY):
+            row_reference(t, den_early[:, t, :], scratch_early[:])
+        for t in range(EARLY):
+            nc.scalar.activation(log_early[:, t, :], den_early[:, t, :], ACT.Ln, scale=inv_ref[:, t : t + 1])
+        for t in range(EARLY):
+            nc.scalar.activation(rel[t][:], log_early[:, t, :], ACT.Exp, scale=-1.0)
 
-        w1dw, w1ds = deal(w1w, w1s, "w1d", "held")
+        w1dw = placed.tile([P, 2 * H], U8, name="w1dw", offset=32768, align_bytes=64)
+        deal_words(w1w, w1dw)
         xgs = keep.tile([P, S], U8, name="xgs", align_bytes=64)
         nc.vector.tensor_copy(xgs[:], xs[:].indirect(offs_sb[:]))
-        xgw = []
+        w1ds = placed.tile([P, H], U8, name="w1ds", offset=57344, align_bytes=64)
+        deal_scales(w1s, w1ds)
+        xds = keep.tile([P, S], U8, name="xds", align_bytes=64)
+        nc.vector.tensor_copy(
+            out=xds[:].rearrange("p (h d v) -> p h v d", h=2, d=D), in_=xgs[:].rearrange("p (h v d) -> p h v d", h=2, d=D)
+        )
+        xgw, xdw = [], []
         for h in range(2):
             g = keep.tile([P, HALF], U32, name="xgw%d" % h, align_bytes=64)
             nc.vector.tensor_copy(g[:], xw[:].indirect(offs_sb[:, h * 32 : (h + 1) * 32]))
             xgw.append(g)
+        for h in range(2):
+            g = keep.tile([P, HALF], U32, name="xdw%d" % h, align_bytes=64)
+            nc.vector.tensor_copy(out=g[:].rearrange("p (d v) -> p v d", d=D), in_=xgw[h][:].rearrange("p (v d) -> p v d", d=D))
+            xdw.append(g)
+
+        unit_sb = placed.tile([P, PACK], F32, name="unit_sb", offset=49184)
+        w2w = placed.tile([P, 2 * H], U8, name="w2w", offset=49216)
+        w2s = placed.tile([P, H], U8, name="w2s", offset=50240)
+        w3w = placed.tile([P, 2 * N], U8, name="w3w", align_bytes=64, offset=50752)
+        w3s = placed.tile([P, N], U8, name="w3s", align_bytes=64, offset=51264)
+        den_late = [placed.tile([P, S], F32, name="den%d" % t, offset=o) for t, o in ((2, 20480), (3, 24576))]
+        nc.vector.memset(w2s[:].bitcast(I32), 0)
+        nc.vector.memset(w3s[:].bitcast(I32), 0)
+        nc.sync.dma_start(out=w2w[:].bitcast(I32), in_=w2_words[0].bitcast(I32))
+        load_scale_rows([nc.sync] * 4, w2s, w2_scales[0])
+        nc.sync.dma_start(out=unit_sb[:], in_=unit.rearrange("(p t) o -> p (t o)", t=PACK))
+        for t in range(EARLY, PACK):
+            nc.sync.dma_start(out=den_late[t - EARLY][:], in_=den_rows[:, t, :])
+        nc.sync.dma_start(out=w3w[:].bitcast(I32), in_=w3_words[0].bitcast(I32))
+        load_scale_rows([nc.sync] * 4, w3s, w3_scales[0])
 
         def product(bank, dw, ds, t, h):
             nc.tensor.matmul_mx(
@@ -116,70 +140,155 @@ def tile_picked_yrloov_pen_p_kernel(
                 stop=True,
             )
 
-        rew = [keep.tile([P, S], F32, name="rew%d" % t) for t in range(PACK)]
-        for t in range(PACK):
+        def new_bank():
+            return psum.tile([P, HALF], F32, name="bank", bufs=6)
+
+        rew = [keep.tile([P, S], F32, name="rew%d" % t) for t in range(DIRECT)]
+        for t in range(DIRECT):
             for h in range(2):
-                bank = psum.tile([P, HALF], F32, name="y", bufs=3)
+                bank = new_bank()
                 product(bank, w1dw, w1ds, t, h)
                 nc.scalar.activation(rew[t][:, h * HALF : (h + 1) * HALF], bank[:], ACT.Sigmoid)
 
-        w2dw, w2ds = deal(w2w, w2s, "w2d", "w2dw")
-        for t in range(1, PACK):
-            row_reference(t)
-        nc.vector.tensor_tensor(base_gain[:], inv_ref[:], unit_sb[:], ALU.mult)
+        turned_cols = (PACK - DIRECT) * P
+        rew_turned = {}
+        for h in range(2):
+            for d in range(D):
+                bank = new_bank()
+                c0 = 0
+                for n in TURNED_WIDTHS:
+                    w0 = DIRECT * P + c0
+                    nc.tensor.matmul_mx(
+                        out=bank[:, c0 : c0 + n],
+                        lhsT=xdw[h][:, d * P : (d + 1) * P].bitcast(FP8X4),
+                        lhsT_scale=xds[:, h * HALF + d * P : h * HALF + (d + 1) * P],
+                        rhs=w1dw[:, 2 * w0 : 2 * (w0 + n)].bitcast(FP4X4),
+                        rhs_scale=w1ds[:, w0 : w0 + n],
+                        start=True,
+                        stop=True,
+                    )
+                    c0 = c0 + n
+                r = keep.tile([P, turned_cols], F32, name="rewT%d%d" % (h, d))
+                nc.scalar.activation(r[:], bank[:, 0:turned_cols], ACT.Sigmoid)
+                rew_turned[h, d] = r
+
+        w2dw = placed.tile([P, 2 * H], U8, name="w2dw", offset=4 * T - 512, align_bytes=64)
+        w2ds = placed.tile([P, H], U8, name="w2ds", offset=0, align_bytes=64)
+        deal_words(w2w, w2dw)
+        deal_scales(w2s, w2ds)
+        nc.vector.tensor_tensor(base_gain[:, 0:EARLY], inv_ref[:, 0:EARLY], unit_sb[:, 0:EARLY], ALU.mult)
         nc.vector.tensor_scalar(sq_gain[:], unit_sb[:], -0.15, None, ALU.mult)
 
-        logs = keep.tile([P, PACK - 1, S], F32, name="logs", tag="held", align_bytes=64)
-        for t in range(1, PACK):
-            nc.scalar.activation(logs[:, t - 1, :], den_sb[t][:], ACT.Ln, scale=inv_ref[:, t : t + 1])
-        for t in range(1, PACK):
-            nc.scalar.activation(rel[t][:], logs[:, t - 1, :], ACT.Exp, scale=-1.0)
-
+        adv = [keep.tile([P, S], F32, name="adv%d" % t) for t in range(PACK)]
+        pgz = keep.tile([P, PACK, S], F32, name="pgz")
+        hid = keep.tile([P, PACK, S], F32, name="hid")
         others = []
-        for t in range(PACK):
-            pair = work.tile([P, S // 2], F32, name="pair")
-            two = rew[t][:].rearrange("p (g e) -> p g e", e=2)
-            nc.vector.tensor_tensor(pair[:], two[:, :, 0], two[:, :, 1], ALU.add)
+        for t in range(DIRECT):
+            pair = work.tile([P, 2, HALF // 2], F32, name="pair")
             oth = keep.tile([P, S], F32, name="others%d" % t)
-            nc.vector.tensor_tensor(
-                oth[:].rearrange("p (v h e) -> p v h e", h=2, e=2),
-                rew[t][:].rearrange("p (v h e) -> p v h e", h=2, e=2)[:, :, :, ::-1],
-                pair[:].rearrange("p (v h) -> p v h", h=2)[:, :, ::-1].unsqueeze(3).to_broadcast([P, S // D, 2, 2]),
-                ALU.add,
-            )
+            for h in range(2):
+                two = rew[t][:, h * HALF : (h + 1) * HALF].rearrange("p (g e) -> p g e", e=2)
+                nc.vector.tensor_tensor(pair[:, h, :], two[:, :, 0], two[:, :, 1], ALU.add)
+            for h in range(2):
+                cols = slice(h * HALF, (h + 1) * HALF)
+                nc.vector.tensor_tensor(
+                    oth[:, cols].rearrange("p (v g e) -> p v g e", g=2, e=2),
+                    rew[t][:, cols].rearrange("p (v g e) -> p v g e", g=2, e=2)[:, :, :, ::-1],
+                    pair[:, h, :].rearrange("p (v g) -> p v g", g=2)[:, :, ::-1].unsqueeze(3).to_broadcast([P, HALF // D, 2, 2]),
+                    ALU.add,
+                )
             others.append(oth)
 
-        adv = []
-        for t in range(PACK):
+        def late_reciprocals():
+            scratch_late = placed.tile([P, REF], F32, name="scratch_late", offset=1024)
+            for t in range(EARLY, PACK):
+                row_reference(t, den_late[t - EARLY], scratch_late[:])
+            nc.vector.tensor_tensor(base_gain[:, EARLY:PACK], inv_ref[:, EARLY:PACK], unit_sb[:, EARLY:PACK], ALU.mult)
+            log_late = placed.tile([P, PACK - EARLY, S], F32, name="log_late", offset=32768)
+            for t in range(EARLY, PACK):
+                nc.scalar.activation(log_late[:, t - EARLY, :], den_late[t - EARLY][:], ACT.Ln, scale=inv_ref[:, t : t + 1])
+            for t in range(EARLY, PACK):
+                nc.scalar.activation(rel[t][:], log_late[:, t - EARLY, :], ACT.Exp, scale=-1.0)
+
+        def advantage_direct(t):
             base = work.tile([P, S], F32, name="base")
-            nc.vector.scalar_tensor_tensor(base[:], others[t][:], base_gain[:, t : t + 1], rel[t][:], ALU.mult, ALU.mult)
-            a = keep.tile([P, S], F32, name="adv%d" % t)
-            nc.vector.scalar_tensor_tensor(a[:], rew[t][:], unit_sb[:, t : t + 1], base[:], ALU.mult, ALU.subtract)
-            adv.append(a)
+            halves = [slice(h * HALF, (h + 1) * HALF) for h in range(2)]
+            for c in halves:
+                nc.vector.scalar_tensor_tensor(base[:, c], others[t][:, c], base_gain[:, t : t + 1], rel[t][:, c], ALU.mult, ALU.mult)
+            for c in halves:
+                nc.vector.scalar_tensor_tensor(adv[t][:, c], rew[t][:, c], unit_sb[:, t : t + 1], base[:, c], ALU.mult, ALU.subtract)
 
-        pgz = keep.tile([P, PACK, S], F32, name="pgz")
+        def turn(t, h):
+            rows = slice((t - DIRECT) * P, (t - DIRECT + 1) * P)
+            rest, own = new_bank(), new_bank()
+            for d in range(D):
+                mates = [e for e in range(D) if e != d]
+                for e in mates:
+                    nc.tensor.matmul(
+                        rest[:, d * P : (d + 1) * P], rew_turned[h, e][:, rows], ident[:],
+                        is_transpose=True, start=(e == mates[0]), stop=(e == mates[-1]),
+                    )
+            for d in range(D):
+                nc.tensor.transpose(own[:, d * P : (d + 1) * P], rew_turned[h, d][:, rows], ident[:])
+            return rest, own
 
-        def gradient_term(t, h):
-            cols = slice(h * HALF, (h + 1) * HALF)
-            bank = psum.tile([P, HALF], F32, name="yl", bufs=3)
+        def advantage_turned(t, banks):
+            bases = []
+            for h in range(2):
+                cols = slice(h * HALF, (h + 1) * HALF)
+                base = work.tile([P, HALF], F32, name="base_half")
+                nc.vector.scalar_tensor_tensor(
+                    base[:].rearrange("p (v d) -> p v d", d=D),
+                    banks[h][0][:].rearrange("p (d v) -> p v d", d=D),
+                    base_gain[:, t : t + 1],
+                    rel[t][:, cols].rearrange("p (v d) -> p v d", d=D),
+                    ALU.mult,
+                    ALU.mult,
+                )
+                bases.append(base)
+            for h in range(2):
+                cols = slice(h * HALF, (h + 1) * HALF)
+                nc.vector.scalar_tensor_tensor(
+                    adv[t][:, cols].rearrange("p (v d) -> p v d", d=D),
+                    banks[h][1][:].rearrange("p (d v) -> p v d", d=D),
+                    unit_sb[:, t : t + 1],
+                    bases[h][:].rearrange("p (v d) -> p v d", d=D),
+                    ALU.mult,
+                    ALU.subtract,
+                )
+
+        def log_prob(t, h):
+            bank = psum.tile([P, HALF], F32, name="yl", bufs=2)
             product(bank, w2dw, w2ds, t, h)
-            sq = work.tile([P, HALF], F32, name="sq", bufs=3)
+            sq = work.tile([P, HALF], F32, name="sq", bufs=4)
             nc.scalar.activation(sq[:], bank[:], ACT.Square)
-            pos = work.tile([P, HALF], F32, name="pos", bufs=3)
-            nc.vector.scalar_tensor_tensor(pos[:], bank[:], 0.0, adv[t][:, cols], ALU.max, ALU.mult)
-            nc.vector.scalar_tensor_tensor(pgz[:, t, cols], sq[:], sq_gain[:, t : t + 1], pos[:], ALU.mult, ALU.add)
+            return bank, sq
+
+        def gradient_terms(t, made):
+            pos = []
+            for h in range(2):
+                cols = slice(h * HALF, (h + 1) * HALF)
+                p = work.tile([P, HALF], F32, name="pos", bufs=3)
+                nc.vector.scalar_tensor_tensor(p[:], made[h][0][:], 0.0, adv[t][:, cols], ALU.max, ALU.mult)
+                pos.append(p)
+            for h in range(2):
+                cols = slice(h * HALF, (h + 1) * HALF)
+                nc.vector.scalar_tensor_tensor(pgz[:, t, cols], made[h][1][:], sq_gain[:, t : t + 1], pos[h][:], ALU.mult, ALU.add)
+
+        def fetch(t, c0, n):
+            nc.vector.tensor_tensor(
+                hid[:, t, c0 : c0 + n], adv[t][:].indirect(shuf_sb[:, c0 // 16 : (c0 + n) // 16]), pgz[:, t, c0 : c0 + n], ALU.add
+            )
 
         out_rows = out.rearrange("(a p) j -> p a j", p=P)
 
-        def finish(c0, n):
-            hid = keep.tile([P, PACK, n], F32, name="hid%d" % c0)
-            for t in range(PACK):
-                nc.vector.tensor_tensor(
-                    hid[:, t, :], adv[t][:].indirect(shuf_sb[:, c0 // 16 : (c0 + n) // 16]), pgz[:, t, c0 : c0 + n], ALU.add
-                )
+        def weave(c0, n):
             grouped = keep.tile([P, n * PACK], BF16, name="grouped%d" % c0, align_bytes=64)
-            weave = nc.vector.tensor_copy if c0 + n == S else nc.scalar.copy
-            weave(grouped[:].rearrange("p (c i t) -> p c t i", i=4, t=PACK), hid[:].rearrange("p t (c i) -> p c t i", i=4))
+            copy = nc.vector.tensor_copy if c0 + n == S else nc.scalar.copy
+            copy(grouped[:].rearrange("p (c i t) -> p c t i", i=4, t=PACK), hid[:, :, c0 : c0 + n].rearrange("p t (c i) -> p c t i", i=4))
+            return grouped
+
+        def finish(c0, n, grouped):
             codes = keep.tile([P, n], U32, name="codes%d" % c0, align_bytes=64)
             scales = keep.tile([P, n], U8, name="scales%d" % c0, align_bytes=64)
             nc.vector.quantize_mx(out=codes[:].bitcast(FP8X4), scales=scales[:], in_=grouped[:])
@@ -187,7 +296,7 @@ def tile_picked_yrloov_pen_p_kernel(
             per_bank = min(2, HALF // n)
             for a in range(2):
                 if a % per_bank == 0:
-                    bank = psum.tile([P, HALF], F32, name="o", bufs=2)
+                    bank = new_bank()
                 nc.tensor.matmul_mx(
                     out=bank[:, (a % per_bank) * n : (a % per_bank + 1) * n],
                     lhsT=w3w[:, 2 * P * a : 2 * P * (a + 1)].bitcast(FP4X4),
@@ -201,9 +310,28 @@ def tile_picked_yrloov_pen_p_kernel(
                     nc.scalar.copy(res[:, a + 1 - per_bank : a + 1, :].rearrange("p a j -> p (a j)"), bank[:, 0 : per_bank * n])
             nc.sync.dma_start(out=out_rows[:, :, c0 : c0 + n], in_=res[:])
 
-        for h in range(2):
-            for t in range(PACK):
-                gradient_term(t, h)
-            for c0, n in BLOCKS:
-                if c0 // HALF == h:
-                    finish(c0, n)
+        turned = None
+        for t in range(PACK):
+            made = [log_prob(t, h) for h in range(2)]
+            if t == 0:
+                late_reciprocals()
+            if t < DIRECT:
+                advantage_direct(t)
+            else:
+                advantage_turned(t, turned)
+            if DIRECT <= t + 1 < PACK:
+                turned = [turn(t + 1, h) for h in range(2)]
+            gradient_terms(t, made)
+            if t < PACK - LATE_FETCH:
+                for h in range(2):
+                    fetch(t, h * HALF, HALF)
+
+        waiting = None
+        for c0, n in BLOCKS:
+            for t in range(PACK - LATE_FETCH, PACK):
+                fetch(t, c0, n)
+            grouped = weave(c0, n)
+            if waiting is not None:
+                finish(*waiting)
+            waiting = (c0, n, grouped)
+        finish(*waiting)

@@ -49,21 +49,27 @@ def tile_picked_yrloov_pen_p_kernel(
         den_early = placed.tile([P, EARLY, S], F32, name="den_early", offset=49152)
         xs = placed.tile([P, T], U8, name="xs", offset=57344)
         w1w = keep.tile([P, 2 * H], U8, name="w1w")
-        xw = placed.tile([P, T], U32, name="xw", offset=0)
-        w1s = placed.tile([P, H], U8, name="w1s", offset=4 * T)
+        w1s = keep.tile([P, H], U8, name="w1s")
+        w2w = keep.tile([P, 2 * H], U8, name="w2w")
         log_early = placed.tile([P, EARLY, S], F32, name="log_early", offset=20480)
 
+        warm_in = keep.tile([P, 1], F32, name="warm_in")
+        warm_out = keep.tile([P, 1], F32, name="warm_out")
+        nc.vector.memset(warm_in[:], 1.0)
+        nc.scalar.activation(warm_out[:], warm_in[:], ACT.Ln)
+        xw = placed.tile([P, T], U32, name="xw", offset=0)
+
         nc.vector.memset(xs[:].bitcast(I32), 0)
-        nc.vector.memset(w1s[:].bitcast(I32), 0)
+        nc.gpsimd.memset(w1s[:].bitcast(I32), 0)
 
         nc.sync.dma_start(offs_sb[:], offs)
+        load_scale_rows([nc.sync] * 4, w1s, w1_scales[0])
+        nc.sync.dma_start(out=den_early[:, 0, :], in_=den_rows[:, 0, :])
         nc.sync.dma_start(out=w1w[:].bitcast(I32), in_=w1_words[0].bitcast(I32))
-        nc.sync.dma_start(shuf_sb[:], shuf)
-        for t in range(EARLY):
-            nc.scalar.dma_start(out=den_early[:, t, :], in_=den_rows[:, t, :])
-        nc.scalar.dma_start(out=xw[:].bitcast(I32), in_=x_words[0].rearrange("p n t -> p (n t)").bitcast(I32))
+        nc.sync.dma_start(out=den_early[:, 1, :], in_=den_rows[:, 1, :])
+        nc.sync.dma_start(out=w2w[:].bitcast(I32), in_=w2_words[0].bitcast(I32))
         load_scale_rows([nc.sync] * 4, xs, x_scales[0])
-        load_scale_rows([nc.sync, nc.sync, nc.gpsimd, nc.gpsimd], w1s, w1_scales[0])
+        nc.sync.dma_start(out=xw[:].bitcast(I32), in_=x_words[0].rearrange("p n t -> p (n t)").bitcast(I32))
         ident = keep.tile([P, P], F32, name="ident")
         make_identity(nc, ident[:])
 
@@ -71,61 +77,62 @@ def tile_picked_yrloov_pen_p_kernel(
         mean_ref = keep.tile([P, PACK], F32, name="mean_ref")
         base_gain = keep.tile([P, PACK], F32, name="base_gain")
         sq_gain = keep.tile([P, PACK], F32, name="sq_gain")
-        rel = [keep.tile([P, S], F32, name="rel%d" % t) for t in range(PACK)]
+        rel_early = keep.tile([P, EARLY, S], F32, name="rel_early")
+        rel_late = keep.tile([P, PACK - EARLY, S], F32, name="rel_late")
+        rel = [rel_early[:, t, :] for t in range(EARLY)] + [rel_late[:, t, :] for t in range(PACK - EARLY)]
 
-        def row_reference(t, rows, scratch):
+        def row_mean(t, rows, scratch):
             nc.vector.tensor_scalar(scratch, rows[:, 0:REF], 1.0 / REF, 0.0, ALU.mult, ALU.add, accum_out=mean_ref[:, t : t + 1])
-            nc.vector.reciprocal(inv_ref[:, t : t + 1], mean_ref[:, t : t + 1])
 
         def deal_words(words, dw):
             nc.vector.tensor_copy(
                 out=dw[:].rearrange("p (t m b) -> p t m b", t=PACK, b=2), in_=words[:].rearrange("p (m t b) -> p t m b", t=PACK, b=2)
             )
 
-        def deal_scales(scales, ds):
-            nc.vector.tensor_copy(out=ds[:].rearrange("p (t m) -> p t m", t=PACK), in_=scales[:].rearrange("p (m t) -> p t m", t=PACK))
+        def deal_scales(scales, ds, t0, t1):
+            nc.vector.tensor_copy(
+                out=ds[:].rearrange("p (t m) -> p t m", t=PACK)[:, t0:t1, :], in_=scales[:].rearrange("p (m t) -> p t m", t=PACK)[:, t0:t1, :]
+            )
 
         scratch_early = keep.tile([P, REF], F32, name="scratch_early")
         for t in range(EARLY):
-            row_reference(t, den_early[:, t, :], scratch_early[:])
+            row_mean(t, den_early[:, t, :], scratch_early[:])
+            nc.vector.reciprocal(inv_ref[:, t : t + 1], mean_ref[:, t : t + 1])
         for t in range(EARLY):
             nc.scalar.activation(log_early[:, t, :], den_early[:, t, :], ACT.Ln, scale=inv_ref[:, t : t + 1])
-        for t in range(EARLY):
-            nc.scalar.activation(rel[t][:], log_early[:, t, :], ACT.Exp, scale=-1.0)
+        nc.scalar.activation(rel_early[:], log_early[:], ACT.Exp, scale=-1.0)
 
         w1dw = placed.tile([P, 2 * H], U8, name="w1dw", offset=32768, align_bytes=64)
         deal_words(w1w, w1dw)
+        w1ds = keep.tile([P, H], U8, name="w1ds", align_bytes=64)
+        deal_scales(w1s, w1ds, 0, PACK)
         xgs = keep.tile([P, S], U8, name="xgs", align_bytes=64)
         nc.vector.tensor_copy(xgs[:], xs[:].indirect(offs_sb[:]))
-        w1ds = placed.tile([P, H], U8, name="w1ds", offset=57344, align_bytes=64)
-        deal_scales(w1s, w1ds)
         xds = keep.tile([P, S], U8, name="xds", align_bytes=64)
         nc.vector.tensor_copy(
             out=xds[:].rearrange("p (h d v) -> p h v d", h=2, d=D), in_=xgs[:].rearrange("p (h v d) -> p h v d", h=2, d=D)
         )
-        xgw, xdw = [], []
+        w2dw = keep.tile([P, 2 * H], U8, name="w2dw", align_bytes=64)
+        deal_words(w2w, w2dw)
+        xgw = [keep.tile([P, HALF], U32, name="xgw%d" % h, align_bytes=64) for h in range(2)]
+        xdw = [keep.tile([P, HALF], U32, name="xdw%d" % h, align_bytes=64) for h in range(2)]
+        nc.vector.tensor_copy(xgw[0][:], xw[:].indirect(offs_sb[:, 0:32]))
+        nc.vector.tensor_copy(xgw[1][:], xw[:].indirect(offs_sb[:, 32:64]))
         for h in range(2):
-            g = keep.tile([P, HALF], U32, name="xgw%d" % h, align_bytes=64)
-            nc.vector.tensor_copy(g[:], xw[:].indirect(offs_sb[:, h * 32 : (h + 1) * 32]))
-            xgw.append(g)
-        for h in range(2):
-            g = keep.tile([P, HALF], U32, name="xdw%d" % h, align_bytes=64)
-            nc.vector.tensor_copy(out=g[:].rearrange("p (d v) -> p v d", d=D), in_=xgw[h][:].rearrange("p (v d) -> p v d", d=D))
-            xdw.append(g)
+            nc.vector.tensor_copy(out=xdw[h][:].rearrange("p (d v) -> p v d", d=D), in_=xgw[h][:].rearrange("p (v d) -> p v d", d=D))
 
         unit_sb = placed.tile([P, PACK], F32, name="unit_sb", offset=49184)
-        w2w = placed.tile([P, 2 * H], U8, name="w2w", offset=49216)
         w2s = placed.tile([P, H], U8, name="w2s", offset=50240)
         w3w = placed.tile([P, 2 * N], U8, name="w3w", align_bytes=64, offset=50752)
         w3s = placed.tile([P, N], U8, name="w3s", align_bytes=64, offset=51264)
         den_late = [placed.tile([P, S], F32, name="den%d" % t, offset=o) for t, o in ((2, 20480), (3, 24576))]
         nc.vector.memset(w2s[:].bitcast(I32), 0)
         nc.vector.memset(w3s[:].bitcast(I32), 0)
-        nc.sync.dma_start(out=w2w[:].bitcast(I32), in_=w2_words[0].bitcast(I32))
         load_scale_rows([nc.sync] * 4, w2s, w2_scales[0])
         nc.sync.dma_start(out=unit_sb[:], in_=unit.rearrange("(p t) o -> p (t o)", t=PACK))
         for t in range(EARLY, PACK):
             nc.sync.dma_start(out=den_late[t - EARLY][:], in_=den_rows[:, t, :])
+        nc.sync.dma_start(shuf_sb[:], shuf)
         nc.sync.dma_start(out=w3w[:].bitcast(I32), in_=w3_words[0].bitcast(I32))
         load_scale_rows([nc.sync] * 4, w3s, w3_scales[0])
 
@@ -172,10 +179,8 @@ def tile_picked_yrloov_pen_p_kernel(
                 nc.scalar.activation(r[:], bank[:, 0:turned_cols], ACT.Sigmoid)
                 rew_turned[h, d] = r
 
-        w2dw = placed.tile([P, 2 * H], U8, name="w2dw", offset=4 * T - 512, align_bytes=64)
         w2ds = placed.tile([P, H], U8, name="w2ds", offset=0, align_bytes=64)
-        deal_words(w2w, w2dw)
-        deal_scales(w2s, w2ds)
+        deal_scales(w2s, w2ds, 0, PACK)
         nc.vector.tensor_tensor(base_gain[:, 0:EARLY], inv_ref[:, 0:EARLY], unit_sb[:, 0:EARLY], ALU.mult)
         nc.vector.tensor_scalar(sq_gain[:], unit_sb[:], -0.15, None, ALU.mult)
 
@@ -184,7 +189,7 @@ def tile_picked_yrloov_pen_p_kernel(
         hid = keep.tile([P, PACK, S], F32, name="hid")
         others = []
         for t in range(DIRECT):
-            pair = work.tile([P, 2, HALF // 2], F32, name="pair")
+            pair = placed.tile([P, 2, HALF // 2], F32, name="pair%d" % t, offset=61440 + 2048 * t)
             oth = keep.tile([P, S], F32, name="others%d" % t)
             for h in range(2):
                 two = rew[t][:, h * HALF : (h + 1) * HALF].rearrange("p (g e) -> p g e", e=2)
@@ -200,15 +205,15 @@ def tile_picked_yrloov_pen_p_kernel(
             others.append(oth)
 
         def late_reciprocals():
-            scratch_late = placed.tile([P, REF], F32, name="scratch_late", offset=1024)
+            scratch_late = placed.tile([P, PACK - EARLY, REF], F32, name="scratch_late", offset=61440)
             for t in range(EARLY, PACK):
-                row_reference(t, den_late[t - EARLY], scratch_late[:])
+                row_mean(t, den_late[t - EARLY], scratch_late[:, t - EARLY, :])
+            nc.vector.reciprocal(inv_ref[:, EARLY:PACK], mean_ref[:, EARLY:PACK])
             nc.vector.tensor_tensor(base_gain[:, EARLY:PACK], inv_ref[:, EARLY:PACK], unit_sb[:, EARLY:PACK], ALU.mult)
             log_late = placed.tile([P, PACK - EARLY, S], F32, name="log_late", offset=32768)
             for t in range(EARLY, PACK):
                 nc.scalar.activation(log_late[:, t - EARLY, :], den_late[t - EARLY][:], ACT.Ln, scale=inv_ref[:, t : t + 1])
-            for t in range(EARLY, PACK):
-                nc.scalar.activation(rel[t][:], log_late[:, t - EARLY, :], ACT.Exp, scale=-1.0)
+            nc.scalar.activation(rel_late[:], log_late[:], ACT.Exp, scale=-1.0)
 
         def advantage_direct(t):
             base = work.tile([P, S], F32, name="base")
@@ -284,7 +289,7 @@ def tile_picked_yrloov_pen_p_kernel(
 
         def weave(c0, n):
             grouped = keep.tile([P, n * PACK], BF16, name="grouped%d" % c0, align_bytes=64)
-            copy = nc.vector.tensor_copy if c0 + n == S else nc.scalar.copy
+            copy = nc.vector.tensor_copy if n == P else nc.scalar.copy
             copy(grouped[:].rearrange("p (c i t) -> p c t i", i=4, t=PACK), hid[:, :, c0 : c0 + n].rearrange("p t (c i) -> p c t i", i=4))
             return grouped
 
@@ -307,7 +312,8 @@ def tile_picked_yrloov_pen_p_kernel(
                     stop=True,
                 )
                 if (a + 1) % per_bank == 0:
-                    nc.scalar.copy(res[:, a + 1 - per_bank : a + 1, :].rearrange("p a j -> p (a j)"), bank[:, 0 : per_bank * n])
+                    empty = nc.vector.tensor_copy if c0 + n == S else nc.scalar.copy
+                    empty(res[:, a + 1 - per_bank : a + 1, :].rearrange("p a j -> p (a j)"), bank[:, 0 : per_bank * n])
             nc.sync.dma_start(out=out_rows[:, :, c0 : c0 + n], in_=res[:])
 
         turned = None

@@ -18,19 +18,16 @@ ALU = mybir.AluOpType
 ACT = mybir.ActivationFunctionType
 
 P = 128
-PACK = 4
+TILES = 4
 HALF = 512
+HALVES = (slice(0, HALF), slice(HALF, S))
+PENALTY = 0.15
 REF = 32
-DIRECT = 1
 EARLY = 2
-LATE_FETCH = 2
 TURNED_WIDTHS = (256, 128)
+LATE_FETCH = 2
 BLOCKS = ((0, 256), (256, 256), (512, 256), (768, 128), (896, 128))
-
-
-def load_scale_rows(queues, plane, rows):
-    for q in range(4):
-        queues[q].dma_start(out=plane[32 * q : 32 * q + 4, :].bitcast(I32), in_=rows[4 * q : 4 * q + 4, :].bitcast(I32))
+WORK_BANKS = 6
 
 
 def tile_picked_yrloov_pen_p_kernel(
@@ -39,305 +36,283 @@ def tile_picked_yrloov_pen_p_kernel(
     nc = tc.nc
     with ExitStack() as ctx:
         keep = ctx.enter_context(tc.tile_pool(name="keep", bufs=1))
-        placed = ctx.enter_context(tc.tile_pool(name="placed", bufs=1))
         work = ctx.enter_context(tc.tile_pool(name="work", bufs=2))
         psum = ctx.enter_context(tc.psum_pool(name="psum", bufs=1))
 
-        den_rows = den.rearrange("(p t) j -> p t j", t=PACK)
         offs_sb = keep.tile([P, S // 16], U16, name="offs_sb")
         shuf_sb = keep.tile([P, S // 16], U16, name="shuf_sb")
-        den_early = placed.tile([P, EARLY, S], F32, name="den_early", offset=49152)
-        xs = placed.tile([P, T], U8, name="xs", offset=57344)
-        w1w = keep.tile([P, 2 * H], U8, name="w1w")
-        w1s = keep.tile([P, H], U8, name="w1s")
-        w2w = keep.tile([P, 2 * H], U8, name="w2w")
-        log_early = placed.tile([P, EARLY, S], F32, name="log_early", offset=20480)
+        den_head = keep.tile([P, TILES, REF], F32, name="den_head")
+        den_sb = [keep.tile([P, S], F32, name="den%d" % t) for t in range(TILES)]
+        unit_sb = keep.tile([P, TILES], F32, name="unit_sb")
+        x_w = keep.tile([P, T], U32, name="x_w")
+        x_s = keep.tile([P, T], U8, name="x_s")
+        w1_w = keep.tile([P, 2 * H], U8, name="w1_w")
+        w1_s = keep.tile([P, H], U8, name="w1_s")
+        w2_w = keep.tile([P, 2 * H], U8, name="w2_w")
+        w2_s = keep.tile([P, H], U8, name="w2_s")
+        w3_w = keep.tile([P, 2 * N], U8, name="w3_w", align_bytes=64)
+        w3_s = keep.tile([P, N], U8, name="w3_s", align_bytes=64)
+        scale_rows = keep.tile([P, 2 * S + 2 * H], U8, name="scale_rows", align_bytes=64)
 
         warm_in = keep.tile([P, 1], F32, name="warm_in")
         warm_out = keep.tile([P, 1], F32, name="warm_out")
         nc.vector.memset(warm_in[:], 1.0)
         nc.scalar.activation(warm_out[:], warm_in[:], ACT.Ln)
-        xw = placed.tile([P, T], U32, name="xw", offset=0)
 
-        nc.vector.memset(xs[:].bitcast(I32), 0)
-        nc.gpsimd.memset(w1s[:].bitcast(I32), 0)
+        nc.vector.memset(x_s[:].bitcast(I32), 0)
+        nc.vector.memset(scale_rows[:].bitcast(I32), 0)
+        nc.gpsimd.memset(w1_s[:].bitcast(I32), 0)
+        nc.gpsimd.memset(w2_s[:].bitcast(I32), 0)
 
+        den_rows = den.rearrange("(p t) j -> p t j", t=TILES)
         nc.sync.dma_start(offs_sb[:], offs)
-        load_scale_rows([nc.sync] * 4, w1s, w1_scales[0])
-        nc.sync.dma_start(out=den_early[:, 0, :], in_=den_rows[:, 0, :])
-        nc.sync.dma_start(out=w1w[:].bitcast(I32), in_=w1_words[0].bitcast(I32))
-        nc.sync.dma_start(out=den_early[:, 1, :], in_=den_rows[:, 1, :])
-        nc.sync.dma_start(out=w2w[:].bitcast(I32), in_=w2_words[0].bitcast(I32))
-        load_scale_rows([nc.sync] * 4, xs, x_scales[0])
-        nc.sync.dma_start(out=xw[:].bitcast(I32), in_=x_words[0].rearrange("p n t -> p (n t)").bitcast(I32))
+        nc.sync.dma_start(out=den_sb[0][:], in_=den_rows[:, 0, :])
+        nc.sync.dma_start(out=den_head[:], in_=den_rows[:, :, 0:REF])
+        nc.sync.dma_start(out=x_s[0:P:8, :].bitcast(I32), in_=x_scales[0].bitcast(I32))
+        nc.sync.dma_start(out=den_sb[1][:], in_=den_rows[:, 1, :])
+        nc.sync.dma_start(out=w1_s[0:P:8, :].bitcast(I32), in_=w1_scales[0].bitcast(I32))
+        nc.sync.dma_start(out=w2_s[0:P:8, :].bitcast(I32), in_=w2_scales[0].bitcast(I32))
+        nc.sync.dma_start(out=w1_w[:].bitcast(I32), in_=w1_words[0].bitcast(I32))
+        nc.sync.dma_start(out=w2_w[:].bitcast(I32), in_=w2_words[0].bitcast(I32))
+        nc.sync.dma_start(out=x_w[:].bitcast(I32), in_=x_words[0].rearrange("p n r -> p (n r)").bitcast(I32))
         ident = keep.tile([P, P], F32, name="ident")
         make_identity(nc, ident[:])
 
-        inv_ref = keep.tile([P, PACK], F32, name="inv_ref")
-        mean_ref = keep.tile([P, PACK], F32, name="mean_ref")
-        base_gain = keep.tile([P, PACK], F32, name="base_gain")
-        sq_gain = keep.tile([P, PACK], F32, name="sq_gain")
+        sum_ref = keep.tile([P, TILES], F32, name="sum_ref")
+        mean_ref = keep.tile([P, TILES], F32, name="mean_ref")
+        inv_ref = keep.tile([P, TILES], F32, name="inv_ref")
+        nc.vector.tensor_reduce(sum_ref[:], den_head[:], mybir.AxisListType.X, ALU.add)
+        nc.vector.tensor_scalar(mean_ref[:], sum_ref[:], 1.0 / REF, None, ALU.mult)
+        nc.vector.reciprocal(inv_ref[:], mean_ref[:])
+
+        log_early = keep.tile([P, EARLY, S], F32, name="log_early")
         rel_early = keep.tile([P, EARLY, S], F32, name="rel_early")
-        rel_late = keep.tile([P, PACK - EARLY, S], F32, name="rel_late")
-        rel = [rel_early[:, t, :] for t in range(EARLY)] + [rel_late[:, t, :] for t in range(PACK - EARLY)]
-
-        def row_mean(t, rows, scratch):
-            nc.vector.tensor_scalar(scratch, rows[:, 0:REF], 1.0 / REF, 0.0, ALU.mult, ALU.add, accum_out=mean_ref[:, t : t + 1])
-
-        def deal_words(words, dw):
-            nc.vector.tensor_copy(
-                out=dw[:].rearrange("p (t m b) -> p t m b", t=PACK, b=2), in_=words[:].rearrange("p (m t b) -> p t m b", t=PACK, b=2)
-            )
-
-        def deal_scales(scales, ds, t0, t1):
-            nc.vector.tensor_copy(
-                out=ds[:].rearrange("p (t m) -> p t m", t=PACK)[:, t0:t1, :], in_=scales[:].rearrange("p (m t) -> p t m", t=PACK)[:, t0:t1, :]
-            )
-
-        scratch_early = keep.tile([P, REF], F32, name="scratch_early")
+        rel_late = keep.tile([P, TILES - EARLY, S], F32, name="rel_late")
+        rel = [rel_early[:, t, :] for t in range(EARLY)] + [rel_late[:, t, :] for t in range(TILES - EARLY)]
         for t in range(EARLY):
-            row_mean(t, den_early[:, t, :], scratch_early[:])
-            nc.vector.reciprocal(inv_ref[:, t : t + 1], mean_ref[:, t : t + 1])
-        for t in range(EARLY):
-            nc.scalar.activation(log_early[:, t, :], den_early[:, t, :], ACT.Ln, scale=inv_ref[:, t : t + 1])
+            nc.scalar.activation(log_early[:, t, :], den_sb[t][:], ACT.Ln, scale=inv_ref[:, t : t + 1])
         nc.scalar.activation(rel_early[:], log_early[:], ACT.Exp, scale=-1.0)
 
-        w1dw = placed.tile([P, 2 * H], U8, name="w1dw", offset=32768, align_bytes=64)
-        deal_words(w1w, w1dw)
-        w1ds = keep.tile([P, H], U8, name="w1ds", align_bytes=64)
-        deal_scales(w1s, w1ds, 0, PACK)
-        xgs = keep.tile([P, S], U8, name="xgs", align_bytes=64)
-        nc.vector.tensor_copy(xgs[:], xs[:].indirect(offs_sb[:]))
-        xds = keep.tile([P, S], U8, name="xds", align_bytes=64)
+        picked_s = keep.tile([P, S], U8, name="picked_s")
+        staged = keep.tile([P, 2 * S + 2 * H], U8, name="staged")
+        nc.vector.tensor_copy(picked_s[:], x_s[:].indirect(offs_sb[:]))
+        nc.vector.tensor_copy(out=staged[:, 0:S].bitcast(I32), in_=picked_s[:].bitcast(I32))
         nc.vector.tensor_copy(
-            out=xds[:].rearrange("p (h d v) -> p h v d", h=2, d=D), in_=xgs[:].rearrange("p (h v d) -> p h v d", h=2, d=D)
+            out=staged[:, S : 2 * S].rearrange("p (h d v) -> p h v d", h=2, d=D),
+            in_=picked_s[:].rearrange("p (h v d) -> p h v d", h=2, d=D),
         )
-        w2dw = keep.tile([P, 2 * H], U8, name="w2dw", align_bytes=64)
-        deal_words(w2w, w2dw)
-        xgw = [keep.tile([P, HALF], U32, name="xgw%d" % h, align_bytes=64) for h in range(2)]
-        xdw = [keep.tile([P, HALF], U32, name="xdw%d" % h, align_bytes=64) for h in range(2)]
-        nc.vector.tensor_copy(xgw[0][:], xw[:].indirect(offs_sb[:, 0:32]))
-        nc.vector.tensor_copy(xgw[1][:], xw[:].indirect(offs_sb[:, 32:64]))
+        for n, w_s in enumerate((w1_s, w2_s)):
+            nc.vector.tensor_copy(
+                out=staged[:, 2 * S + n * H : 2 * S + (n + 1) * H].rearrange("p (t m) -> p t m", t=TILES),
+                in_=w_s[:].rearrange("p (m t) -> p t m", t=TILES),
+            )
+        for r in range(4):
+            nc.sync.dma_start(out=scale_rows[r:P:32, :].bitcast(I32), in_=staged[8 * r : P : 32, :].bitcast(I32))
+        picked_scales, dealt_scales = scale_rows[:, 0:S], scale_rows[:, S : 2 * S]
+        w1_ds, w2_ds = scale_rows[:, 2 * S : 2 * S + H], scale_rows[:, 2 * S + H : 2 * S + 2 * H]
+
+        w1_dw = keep.tile([P, 2 * H], U8, name="w1_dw", tag="w1_then_logs", align_bytes=64)
+        w2_dw = keep.tile([P, 2 * H], U8, name="w2_dw", align_bytes=64)
+        for w_w, w_dw in ((w1_w, w1_dw), (w2_w, w2_dw)):
+            nc.vector.tensor_copy(
+                out=w_dw[:].rearrange("p (t m b) -> p t m b", t=TILES, b=2),
+                in_=w_w[:].rearrange("p (m t b) -> p t m b", t=TILES, b=2),
+            )
+
+        picked_w = [keep.tile([P, HALF], U32, name="picked_w%d" % h, align_bytes=64) for h in range(2)]
+        dealt_w = [keep.tile([P, HALF], U32, name="dealt_w%d" % h, align_bytes=64) for h in range(2)]
         for h in range(2):
-            nc.vector.tensor_copy(out=xdw[h][:].rearrange("p (d v) -> p v d", d=D), in_=xgw[h][:].rearrange("p (v d) -> p v d", d=D))
+            nc.vector.tensor_copy(picked_w[h][:], x_w[:].indirect(offs_sb[:, h * HALF // 16 : (h + 1) * HALF // 16]))
+        for h in range(2):
+            nc.vector.tensor_copy(
+                out=dealt_w[h][:].rearrange("p (d v) -> p v d", d=D), in_=picked_w[h][:].rearrange("p (v d) -> p v d", d=D)
+            )
 
-        unit_sb = placed.tile([P, PACK], F32, name="unit_sb", offset=49184)
-        w2s = placed.tile([P, H], U8, name="w2s", offset=50240)
-        w3w = placed.tile([P, 2 * N], U8, name="w3w", align_bytes=64, offset=50752)
-        w3s = placed.tile([P, N], U8, name="w3s", align_bytes=64, offset=51264)
-        den_late = [placed.tile([P, S], F32, name="den%d" % t, offset=o) for t, o in ((2, 20480), (3, 24576))]
-        nc.vector.memset(w2s[:].bitcast(I32), 0)
-        nc.vector.memset(w3s[:].bitcast(I32), 0)
-        load_scale_rows([nc.sync] * 4, w2s, w2_scales[0])
-        nc.sync.dma_start(out=unit_sb[:], in_=unit.rearrange("(p t) o -> p (t o)", t=PACK))
-        for t in range(EARLY, PACK):
-            nc.sync.dma_start(out=den_late[t - EARLY][:], in_=den_rows[:, t, :])
+        nc.vector.memset(w3_s[:].bitcast(I32), 0)
+        nc.sync.dma_start(out=unit_sb[:], in_=unit.rearrange("(p t) o -> p (t o)", t=TILES))
+        for t in range(EARLY, TILES):
+            nc.sync.dma_start(out=den_sb[t][:], in_=den_rows[:, t, :])
         nc.sync.dma_start(shuf_sb[:], shuf)
-        nc.sync.dma_start(out=w3w[:].bitcast(I32), in_=w3_words[0].bitcast(I32))
-        load_scale_rows([nc.sync] * 4, w3s, w3_scales[0])
+        nc.sync.dma_start(out=w3_w[:].bitcast(I32), in_=w3_words[0].bitcast(I32))
+        for q in range(4):
+            nc.sync.dma_start(
+                out=w3_s[32 * q : 32 * q + 4, :].bitcast(I32), in_=w3_scales[0][4 * q : 4 * q + 4, :].bitcast(I32)
+            )
 
-        def product(bank, dw, ds, t, h):
+        def work_bank():
+            return psum.tile([P, HALF], F32, name="bank", bufs=WORK_BANKS)
+
+        def row_product(bank, w_dw, w_ds, t, h):
             nc.tensor.matmul_mx(
                 out=bank[:],
-                lhsT=dw[:, 2 * P * t : 2 * P * (t + 1)].bitcast(FP4X4),
-                lhsT_scale=ds[:, P * t : P * (t + 1)],
-                rhs=xgw[h][:].bitcast(FP8X4),
-                rhs_scale=xgs[:, h * HALF : (h + 1) * HALF],
+                lhsT=w_dw[:, 2 * P * t : 2 * P * (t + 1)].bitcast(FP4X4),
+                lhsT_scale=w_ds[:, P * t : P * (t + 1)],
+                rhs=picked_w[h][:].bitcast(FP8X4),
+                rhs_scale=picked_scales[:, HALVES[h]],
                 start=True,
                 stop=True,
             )
 
-        def new_bank():
-            return psum.tile([P, HALF], F32, name="bank", bufs=6)
+        rew0 = keep.tile([P, S], F32, name="rew0")
+        for h in range(2):
+            bank = work_bank()
+            row_product(bank, w1_dw, w1_ds, 0, h)
+            nc.scalar.activation(rew0[:, HALVES[h]], bank[:], ACT.Sigmoid)
 
-        rew = [keep.tile([P, S], F32, name="rew%d" % t) for t in range(DIRECT)]
-        for t in range(DIRECT):
-            for h in range(2):
-                bank = new_bank()
-                product(bank, w1dw, w1ds, t, h)
-                nc.scalar.activation(rew[t][:, h * HALF : (h + 1) * HALF], bank[:], ACT.Sigmoid)
-
-        turned_cols = (PACK - DIRECT) * P
+        turned_rows = (TILES - 1) * P
         rew_turned = {}
         for h in range(2):
             for d in range(D):
-                bank = new_bank()
+                bank = work_bank()
                 c0 = 0
                 for n in TURNED_WIDTHS:
-                    w0 = DIRECT * P + c0
                     nc.tensor.matmul_mx(
                         out=bank[:, c0 : c0 + n],
-                        lhsT=xdw[h][:, d * P : (d + 1) * P].bitcast(FP8X4),
-                        lhsT_scale=xds[:, h * HALF + d * P : h * HALF + (d + 1) * P],
-                        rhs=w1dw[:, 2 * w0 : 2 * (w0 + n)].bitcast(FP4X4),
-                        rhs_scale=w1ds[:, w0 : w0 + n],
+                        lhsT=dealt_w[h][:, d * P : (d + 1) * P].bitcast(FP8X4),
+                        lhsT_scale=dealt_scales[:, h * HALF + d * P : h * HALF + (d + 1) * P],
+                        rhs=w1_dw[:, 2 * (P + c0) : 2 * (P + c0 + n)].bitcast(FP4X4),
+                        rhs_scale=w1_ds[:, P + c0 : P + c0 + n],
                         start=True,
                         stop=True,
                     )
                     c0 = c0 + n
-                r = keep.tile([P, turned_cols], F32, name="rewT%d%d" % (h, d))
-                nc.scalar.activation(r[:], bank[:, 0:turned_cols], ACT.Sigmoid)
-                rew_turned[h, d] = r
+                rew_turned[h, d] = keep.tile([P, turned_rows], F32, name="rew_turned%d%d" % (h, d))
+                nc.scalar.activation(rew_turned[h, d][:], bank[:, 0:turned_rows], ACT.Sigmoid)
 
-        w2ds = placed.tile([P, H], U8, name="w2ds", offset=0, align_bytes=64)
-        deal_scales(w2s, w2ds, 0, PACK)
-        nc.vector.tensor_tensor(base_gain[:, 0:EARLY], inv_ref[:, 0:EARLY], unit_sb[:, 0:EARLY], ALU.mult)
-        nc.vector.tensor_scalar(sq_gain[:], unit_sb[:], -0.15, None, ALU.mult)
+        base_gain = keep.tile([P, TILES], F32, name="base_gain")
+        penalty_gain = keep.tile([P, TILES], F32, name="penalty_gain")
+        nc.gpsimd.tensor_tensor(base_gain[:], inv_ref[:], unit_sb[:], ALU.mult)
+        nc.gpsimd.tensor_scalar(penalty_gain[:], unit_sb[:], -PENALTY, 0.0, ALU.mult, ALU.add)
 
-        adv = [keep.tile([P, S], F32, name="adv%d" % t) for t in range(PACK)]
-        pgz = keep.tile([P, PACK, S], F32, name="pgz")
-        hid = keep.tile([P, PACK, S], F32, name="hid")
-        others = []
-        for t in range(DIRECT):
-            pair = placed.tile([P, 2, HALF // 2], F32, name="pair%d" % t, offset=61440 + 2048 * t)
-            oth = keep.tile([P, S], F32, name="others%d" % t)
-            for h in range(2):
-                two = rew[t][:, h * HALF : (h + 1) * HALF].rearrange("p (g e) -> p g e", e=2)
-                nc.vector.tensor_tensor(pair[:, h, :], two[:, :, 0], two[:, :, 1], ALU.add)
-            for h in range(2):
-                cols = slice(h * HALF, (h + 1) * HALF)
-                nc.vector.tensor_tensor(
-                    oth[:, cols].rearrange("p (v g e) -> p v g e", g=2, e=2),
-                    rew[t][:, cols].rearrange("p (v g e) -> p v g e", g=2, e=2)[:, :, :, ::-1],
-                    pair[:, h, :].rearrange("p (v g) -> p v g", g=2)[:, :, ::-1].unsqueeze(3).to_broadcast([P, HALF // D, 2, 2]),
-                    ALU.add,
-                )
-            others.append(oth)
+        pairs = keep.tile([P, 2, HALF // 2], F32, name="pairs")
+        others0 = keep.tile([P, S], F32, name="others0")
+        for h in range(2):
+            two = rew0[:, HALVES[h]].rearrange("p (g e) -> p g e", e=2)
+            nc.vector.tensor_tensor(pairs[:, h, :], two[:, :, 0], two[:, :, 1], ALU.add)
+        for h in range(2):
+            nc.vector.tensor_tensor(
+                others0[:, HALVES[h]].rearrange("p (v g e) -> p v g e", g=2, e=2),
+                rew0[:, HALVES[h]].rearrange("p (v g e) -> p v g e", g=2, e=2)[:, :, :, ::-1],
+                pairs[:, h, :].rearrange("p (v g) -> p v g", g=2)[:, :, ::-1].unsqueeze(3).to_broadcast([P, HALF // D, 2, 2]),
+                ALU.add,
+            )
 
-        def late_reciprocals():
-            scratch_late = placed.tile([P, PACK - EARLY, REF], F32, name="scratch_late", offset=61440)
-            for t in range(EARLY, PACK):
-                row_mean(t, den_late[t - EARLY], scratch_late[:, t - EARLY, :])
-            nc.vector.reciprocal(inv_ref[:, EARLY:PACK], mean_ref[:, EARLY:PACK])
-            nc.vector.tensor_tensor(base_gain[:, EARLY:PACK], inv_ref[:, EARLY:PACK], unit_sb[:, EARLY:PACK], ALU.mult)
-            log_late = placed.tile([P, PACK - EARLY, S], F32, name="log_late", offset=32768)
-            for t in range(EARLY, PACK):
-                nc.scalar.activation(log_late[:, t - EARLY, :], den_late[t - EARLY][:], ACT.Ln, scale=inv_ref[:, t : t + 1])
-            nc.scalar.activation(rel_late[:], log_late[:], ACT.Exp, scale=-1.0)
+        adv = [keep.tile([P, S], F32, name="adv%d" % t) for t in range(TILES)]
+        pgz = keep.tile([P, TILES, S], F32, name="pgz")
+        hid = keep.tile([P, TILES, S], F32, name="hid")
 
-        def advantage_direct(t):
-            base = work.tile([P, S], F32, name="base")
-            halves = [slice(h * HALF, (h + 1) * HALF) for h in range(2)]
-            for c in halves:
-                nc.vector.scalar_tensor_tensor(base[:, c], others[t][:, c], base_gain[:, t : t + 1], rel[t][:, c], ALU.mult, ALU.mult)
-            for c in halves:
-                nc.vector.scalar_tensor_tensor(adv[t][:, c], rew[t][:, c], unit_sb[:, t : t + 1], base[:, c], ALU.mult, ALU.subtract)
+        def by_member(ap):
+            return ap.rearrange("p (d v) -> p v d", d=D)
+
+        def by_group(ap):
+            return ap.rearrange("p (v d) -> p v d", d=D)
 
         def turn(t, h):
-            rows = slice((t - DIRECT) * P, (t - DIRECT + 1) * P)
-            rest, own = new_bank(), new_bank()
+            rows = slice((t - 1) * P, t * P)
+            rest, own = work_bank(), work_bank()
             for d in range(D):
                 mates = [e for e in range(D) if e != d]
                 for e in mates:
                     nc.tensor.matmul(
-                        rest[:, d * P : (d + 1) * P], rew_turned[h, e][:, rows], ident[:],
-                        is_transpose=True, start=(e == mates[0]), stop=(e == mates[-1]),
+                        rest[:, d * P : (d + 1) * P],
+                        rew_turned[h, e][:, rows],
+                        ident[:],
+                        is_transpose=True,
+                        start=(e == mates[0]),
+                        stop=(e == mates[-1]),
                     )
             for d in range(D):
                 nc.tensor.transpose(own[:, d * P : (d + 1) * P], rew_turned[h, d][:, rows], ident[:])
-            return rest, own
+            return by_member(rest[:]), by_member(own[:])
 
-        def advantage_turned(t, banks):
-            bases = []
+        def advantage(t, sources):
+            base = work.tile([P, S], F32, name="base")
             for h in range(2):
-                cols = slice(h * HALF, (h + 1) * HALF)
-                base = work.tile([P, HALF], F32, name="base_half")
                 nc.vector.scalar_tensor_tensor(
-                    base[:].rearrange("p (v d) -> p v d", d=D),
-                    banks[h][0][:].rearrange("p (d v) -> p v d", d=D),
-                    base_gain[:, t : t + 1],
-                    rel[t][:, cols].rearrange("p (v d) -> p v d", d=D),
-                    ALU.mult,
-                    ALU.mult,
+                    by_group(base[:, HALVES[h]]), sources[h][0], base_gain[:, t : t + 1], by_group(rel[t][:, HALVES[h]]),
+                    ALU.mult, ALU.mult,
                 )
-                bases.append(base)
             for h in range(2):
-                cols = slice(h * HALF, (h + 1) * HALF)
                 nc.vector.scalar_tensor_tensor(
-                    adv[t][:, cols].rearrange("p (v d) -> p v d", d=D),
-                    banks[h][1][:].rearrange("p (d v) -> p v d", d=D),
-                    unit_sb[:, t : t + 1],
-                    bases[h][:].rearrange("p (v d) -> p v d", d=D),
-                    ALU.mult,
-                    ALU.subtract,
+                    by_group(adv[t][:, HALVES[h]]), sources[h][1], unit_sb[:, t : t + 1], by_group(base[:, HALVES[h]]),
+                    ALU.mult, ALU.subtract,
                 )
 
         def log_prob(t, h):
-            bank = psum.tile([P, HALF], F32, name="yl", bufs=2)
-            product(bank, w2dw, w2ds, t, h)
-            sq = work.tile([P, HALF], F32, name="sq", bufs=4)
-            nc.scalar.activation(sq[:], bank[:], ACT.Square)
-            return bank, sq
+            bank = psum.tile([P, HALF], F32, name="yl", bufs=8 - WORK_BANKS)
+            row_product(bank, w2_dw, w2_ds, t, h)
+            square = work.tile([P, HALF], F32, name="square", bufs=4)
+            nc.scalar.activation(square[:], bank[:], ACT.Square)
+            return bank, square
 
-        def gradient_terms(t, made):
-            pos = []
+        def gradient_terms(t, yl):
+            gated = [work.tile([P, HALF], F32, name="gated", bufs=3) for h in range(2)]
             for h in range(2):
-                cols = slice(h * HALF, (h + 1) * HALF)
-                p = work.tile([P, HALF], F32, name="pos", bufs=3)
-                nc.vector.scalar_tensor_tensor(p[:], made[h][0][:], 0.0, adv[t][:, cols], ALU.max, ALU.mult)
-                pos.append(p)
+                nc.vector.scalar_tensor_tensor(gated[h][:], yl[h][0][:], 0.0, adv[t][:, HALVES[h]], ALU.max, ALU.mult)
             for h in range(2):
-                cols = slice(h * HALF, (h + 1) * HALF)
-                nc.vector.scalar_tensor_tensor(pgz[:, t, cols], made[h][1][:], sq_gain[:, t : t + 1], pos[h][:], ALU.mult, ALU.add)
+                nc.vector.scalar_tensor_tensor(
+                    pgz[:, t, HALVES[h]], yl[h][1][:], penalty_gain[:, t : t + 1], gated[h][:], ALU.mult, ALU.add
+                )
 
         def fetch(t, c0, n):
             nc.vector.tensor_tensor(
                 hid[:, t, c0 : c0 + n], adv[t][:].indirect(shuf_sb[:, c0 // 16 : (c0 + n) // 16]), pgz[:, t, c0 : c0 + n], ALU.add
             )
 
+        def weave(c0, n):
+            woven = keep.tile([P, n * TILES], BF16, name="woven%d" % c0, align_bytes=64)
+            copy = nc.vector.tensor_copy if n == P else nc.scalar.copy
+            copy(
+                woven[:].rearrange("p (c i t) -> p c t i", i=4, t=TILES),
+                hid[:, :, c0 : c0 + n].rearrange("p t (c i) -> p c t i", i=4),
+            )
+            return woven
+
         out_rows = out.rearrange("(a p) j -> p a j", p=P)
 
-        def weave(c0, n):
-            grouped = keep.tile([P, n * PACK], BF16, name="grouped%d" % c0, align_bytes=64)
-            copy = nc.vector.tensor_copy if n == P else nc.scalar.copy
-            copy(grouped[:].rearrange("p (c i t) -> p c t i", i=4, t=PACK), hid[:, :, c0 : c0 + n].rearrange("p t (c i) -> p c t i", i=4))
-            return grouped
-
-        def finish(c0, n, grouped):
+        def finish(c0, n, woven):
             codes = keep.tile([P, n], U32, name="codes%d" % c0, align_bytes=64)
             scales = keep.tile([P, n], U8, name="scales%d" % c0, align_bytes=64)
-            nc.vector.quantize_mx(out=codes[:].bitcast(FP8X4), scales=scales[:], in_=grouped[:])
-            res = keep.tile([P, 2, n], F32, name="res%d" % c0)
-            per_bank = min(2, HALF // n)
-            for a in range(2):
-                if a % per_bank == 0:
-                    bank = new_bank()
+            nc.vector.quantize_mx(out=codes[:].bitcast(FP8X4), scales=scales[:], in_=woven[:])
+            bank = work_bank()
+            for a in range(N // P):
                 nc.tensor.matmul_mx(
-                    out=bank[:, (a % per_bank) * n : (a % per_bank + 1) * n],
-                    lhsT=w3w[:, 2 * P * a : 2 * P * (a + 1)].bitcast(FP4X4),
-                    lhsT_scale=w3s[:, P * a : P * (a + 1)],
+                    out=bank[:, a * n : (a + 1) * n],
+                    lhsT=w3_w[:, 2 * P * a : 2 * P * (a + 1)].bitcast(FP4X4),
+                    lhsT_scale=w3_s[:, P * a : P * (a + 1)],
                     rhs=codes[:].bitcast(FP8X4),
                     rhs_scale=scales[:],
                     start=True,
                     stop=True,
                 )
-                if (a + 1) % per_bank == 0:
-                    empty = nc.vector.tensor_copy if c0 + n == S else nc.scalar.copy
-                    empty(res[:, a + 1 - per_bank : a + 1, :].rearrange("p a j -> p (a j)"), bank[:, 0 : per_bank * n])
-            nc.sync.dma_start(out=out_rows[:, :, c0 : c0 + n], in_=res[:])
+            result = keep.tile([P, N // P, n], F32, name="result%d" % c0)
+            empty = nc.vector.tensor_copy if c0 + n == S else nc.scalar.copy
+            empty(result[:].rearrange("p a j -> p (a j)"), bank[:, 0 : N // P * n])
+            nc.sync.dma_start(out=out_rows[:, :, c0 : c0 + n], in_=result[:])
 
-        turned = None
-        for t in range(PACK):
-            made = [log_prob(t, h) for h in range(2)]
-            if t == 0:
-                late_reciprocals()
-            if t < DIRECT:
-                advantage_direct(t)
-            else:
-                advantage_turned(t, turned)
-            if DIRECT <= t + 1 < PACK:
-                turned = [turn(t + 1, h) for h in range(2)]
-            gradient_terms(t, made)
-            if t < PACK - LATE_FETCH:
+        sources = [(by_group(others0[:, HALVES[h]]), by_group(rew0[:, HALVES[h]])) for h in range(2)]
+        log_late = keep.tile([P, TILES - EARLY, S], F32, name="log_late", tag="w1_then_logs", align_bytes=64)
+        for t in range(TILES):
+            yl = [log_prob(t, h) for h in range(2)]
+            for u in range(EARLY, TILES):
+                if t == 0:
+                    nc.scalar.activation(log_late[:, u - EARLY, :], den_sb[u][:], ACT.Ln, scale=inv_ref[:, u : u + 1])
+                if t == 1:
+                    nc.scalar.activation(rel[u], log_late[:, u - EARLY, :], ACT.Exp, scale=-1.0)
+            advantage(t, sources)
+            if t + 1 < TILES:
+                sources = [turn(t + 1, h) for h in range(2)]
+            gradient_terms(t, yl)
+            if t < TILES - LATE_FETCH:
                 for h in range(2):
                     fetch(t, h * HALF, HALF)
 
         waiting = None
         for c0, n in BLOCKS:
-            for t in range(PACK - LATE_FETCH, PACK):
+            for t in range(TILES - LATE_FETCH, TILES):
                 fetch(t, c0, n)
-            grouped = weave(c0, n)
+            woven = weave(c0, n)
             if waiting is not None:
                 finish(*waiting)
-            waiting = (c0, n, grouped)
+            waiting = (c0, n, woven)
         finish(*waiting)

@@ -54,11 +54,6 @@ def tile_picked_yrloov_pen_p_kernel(
         w3_s = keep.tile([P, N], U8, name="w3_s", align_bytes=64)
         scale_rows = keep.tile([P, 2 * S + 2 * H], U8, name="scale_rows", align_bytes=64)
 
-        warm_in = keep.tile([P, 1], F32, name="warm_in")
-        warm_out = keep.tile([P, 1], F32, name="warm_out")
-        nc.vector.memset(warm_in[:], 1.0)
-        nc.scalar.activation(warm_out[:], warm_in[:], ACT.Ln)
-
         nc.vector.memset(x_s[:].bitcast(I32), 0)
         nc.vector.memset(scale_rows[:].bitcast(I32), 0)
         nc.gpsimd.memset(w1_s[:].bitcast(I32), 0)

from contextlib import ExitStack

import concourse.mybir as mybir
from concourse.masks import make_identity

K, T, S, D, N, H = 512, 4096, 1024, 4, 256, 512
FLOPS = 2 * S * (2 * K * H + H * N)

F32 = mybir.dt.float32
BF16 = mybir.dt.bfloat16
I32 = mybir.dt.int32
U32 = mybir.dt.uint32
U16 = mybir.dt.uint16
U8 = mybir.dt.uint8
FP8X4 = mybir.dt.float8_e4m3fn_x4
FP4X4 = mybir.dt.float4_e2m1fn_x4
ALU = mybir.AluOpType
ACT = mybir.ActivationFunctionType

P = 128
TILES = 4
HALF = 512
HALVES = (slice(0, HALF), slice(HALF, S))
PENALTY = 0.15
REF = 32
EARLY = 2
TURNED_WIDTHS = (256, 128)
LATE_FETCH = 2
BLOCKS = ((0, 256), (256, 256), (512, 256), (768, 128), (896, 128))
WORK_BANKS = 6


def tile_picked_yrloov_pen_p_kernel(
    tc, x_words, x_scales, w1_words, w1_scales, w2_words, w2_scales, den, unit, w3_words, w3_scales, offs, shuf, out
):
    nc = tc.nc
    with ExitStack() as ctx:
        keep = ctx.enter_context(tc.tile_pool(name="keep", bufs=1))
        work = ctx.enter_context(tc.tile_pool(name="work", bufs=2))
        psum = ctx.enter_context(tc.psum_pool(name="psum", bufs=1))

        offs_sb = keep.tile([P, S // 16], U16, name="offs_sb")
        shuf_sb = keep.tile([P, S // 16], U16, name="shuf_sb")
        den_head = keep.tile([P, TILES, REF], F32, name="den_head")
        den_sb = [keep.tile([P, S], F32, name="den%d" % t) for t in range(TILES)]
        unit_sb = keep.tile([P, TILES], F32, name="unit_sb")
        x_w = keep.tile([P, T], U32, name="x_w")
        x_s = keep.tile([P, T], U8, name="x_s")
        w1_w = keep.tile([P, 2 * H], U8, name="w1_w")
        w1_s = keep.tile([P, H], U8, name="w1_s")
        w2_w = keep.tile([P, 2 * H], U8, name="w2_w")
        w2_s = keep.tile([P, H], U8, name="w2_s")
        w3_w = keep.tile([P, 2 * N], U8, name="w3_w", align_bytes=64)
        w3_s = keep.tile([P, N], U8, name="w3_s", align_bytes=64)
        scale_rows = keep.tile([P, 2 * S + 2 * H], U8, name="scale_rows", align_bytes=64)

        nc.vector.memset(x_s[:].bitcast(I32), 0)
        nc.vector.memset(scale_rows[:].bitcast(I32), 0)
        nc.gpsimd.memset(w1_s[:].bitcast(I32), 0)
        nc.gpsimd.memset(w2_s[:].bitcast(I32), 0)

        den_rows = den.rearrange("(p t) j -> p t j", t=TILES)
        nc.sync.dma_start(offs_sb[:], offs)
        nc.sync.dma_start(out=den_sb[0][:], in_=den_rows[:, 0, :])
        nc.sync.dma_start(out=den_head[:], in_=den_rows[:, :, 0:REF])
        nc.sync.dma_start(out=x_s[0:P:8, :].bitcast(I32), in_=x_scales[0].bitcast(I32))
        nc.sync.dma_start(out=den_sb[1][:], in_=den_rows[:, 1, :])
        nc.sync.dma_start(out=w1_s[0:P:8, :].bitcast(I32), in_=w1_scales[0].bitcast(I32))
        nc.sync.dma_start(out=w2_s[0:P:8, :].bitcast(I32), in_=w2_scales[0].bitcast(I32))
        nc.sync.dma_start(out=w1_w[:].bitcast(I32), in_=w1_words[0].bitcast(I32))
        nc.sync.dma_start(out=w2_w[:].bitcast(I32), in_=w2_words[0].bitcast(I32))
        nc.sync.dma_start(out=x_w[:].bitcast(I32), in_=x_words[0].rearrange("p n r -> p (n r)").bitcast(I32))
        ident = keep.tile([P, P], F32, name="ident")
        make_identity(nc, ident[:])

        sum_ref = keep.tile([P, TILES], F32, name="sum_ref")
        mean_ref = keep.tile([P, TILES], F32, name="mean_ref")
        inv_ref = keep.tile([P, TILES], F32, name="inv_ref")
        nc.vector.tensor_reduce(sum_ref[:], den_head[:], mybir.AxisListType.X, ALU.add)
        nc.vector.tensor_scalar(mean_ref[:], sum_ref[:], 1.0 / REF, None, ALU.mult)
        nc.vector.reciprocal(inv_ref[:], mean_ref[:])

        log_early = keep.tile([P, EARLY, S], F32, name="log_early")
        rel_early = keep.tile([P, EARLY, S], F32, name="rel_early")
        rel_late = keep.tile([P, TILES - EARLY, S], F32, name="rel_late")
        rel = [rel_early[:, t, :] for t in range(EARLY)] + [rel_late[:, t, :] for t in range(TILES - EARLY)]
        for t in range(EARLY):
            nc.scalar.activation(log_early[:, t, :], den_sb[t][:], ACT.Ln, scale=inv_ref[:, t : t + 1])
        nc.scalar.activation(rel_early[:], log_early[:], ACT.Exp, scale=-1.0)

        picked_s = keep.tile([P, S], U8, name="picked_s")
        staged = keep.tile([P, 2 * S + 2 * H], U8, name="staged")
        nc.vector.tensor_copy(picked_s[:], x_s[:].indirect(offs_sb[:]))
        nc.vector.tensor_copy(out=staged[:, 0:S].bitcast(I32), in_=picked_s[:].bitcast(I32))
        nc.vector.tensor_copy(
            out=staged[:, S : 2 * S].rearrange("p (h d v) -> p h v d", h=2, d=D),
            in_=picked_s[:].rearrange("p (h v d) -> p h v d", h=2, d=D),
        )
        for n, w_s in enumerate((w1_s, w2_s)):
            nc.vector.tensor_copy(
                out=staged[:, 2 * S + n * H : 2 * S + (n + 1) * H].rearrange("p (t m) -> p t m", t=TILES),
                in_=w_s[:].rearrange("p (m t) -> p t m", t=TILES),
            )
        for r in range(4):
            nc.sync.dma_start(out=scale_rows[r:P:32, :].bitcast(I32), in_=staged[8 * r : P : 32, :].bitcast(I32))
        picked_scales, dealt_scales = scale_rows[:, 0:S], scale_rows[:, S : 2 * S]
        w1_ds, w2_ds = scale_rows[:, 2 * S : 2 * S + H], scale_rows[:, 2 * S + H : 2 * S + 2 * H]

        w1_dw = keep.tile([P, 2 * H], U8, name="w1_dw", tag="w1_then_logs", align_bytes=64)
        w2_dw = keep.tile([P, 2 * H], U8, name="w2_dw", align_bytes=64)
        for w_w, w_dw in ((w1_w, w1_dw), (w2_w, w2_dw)):
            nc.vector.tensor_copy(
                out=w_dw[:].rearrange("p (t m b) -> p t m b", t=TILES, b=2),
                in_=w_w[:].rearrange("p (m t b) -> p t m b", t=TILES, b=2),
            )

        picked_w = [keep.tile([P, HALF], U32, name="picked_w%d" % h, align_bytes=64) for h in range(2)]
        dealt_w = [keep.tile([P, HALF], U32, name="dealt_w%d" % h, align_bytes=64) for h in range(2)]
        for h in range(2):
            nc.vector.tensor_copy(picked_w[h][:], x_w[:].indirect(offs_sb[:, h * HALF // 16 : (h + 1) * HALF // 16]))
        for h in range(2):
            nc.vector.tensor_copy(
                out=dealt_w[h][:].rearrange("p (d v) -> p v d", d=D), in_=picked_w[h][:].rearrange("p (v d) -> p v d", d=D)
            )

        nc.vector.memset(w3_s[:].bitcast(I32), 0)
        nc.sync.dma_start(out=unit_sb[:], in_=unit.rearrange("(p t) o -> p (t o)", t=TILES))
        for t in range(EARLY, TILES):
            nc.sync.dma_start(out=den_sb[t][:], in_=den_rows[:, t, :])
        nc.sync.dma_start(shuf_sb[:], shuf)
        nc.sync.dma_start(out=w3_w[:].bitcast(I32), in_=w3_words[0].bitcast(I32))
        for q in range(4):
            nc.sync.dma_start(
                out=w3_s[32 * q : 32 * q + 4, :].bitcast(I32), in_=w3_scales[0][4 * q : 4 * q + 4, :].bitcast(I32)
            )

        def work_bank():
            return psum.tile([P, HALF], F32, name="bank", bufs=WORK_BANKS)

        def row_product(bank, w_dw, w_ds, t, h):
            nc.tensor.matmul_mx(
                out=bank[:],
                lhsT=w_dw[:, 2 * P * t : 2 * P * (t + 1)].bitcast(FP4X4),
                lhsT_scale=w_ds[:, P * t : P * (t + 1)],
                rhs=picked_w[h][:].bitcast(FP8X4),
                rhs_scale=picked_scales[:, HALVES[h]],
                start=True,
                stop=True,
            )

        rew0 = keep.tile([P, S], F32, name="rew0")
        for h in range(2):
            bank = work_bank()
            row_product(bank, w1_dw, w1_ds, 0, h)
            nc.scalar.activation(rew0[:, HALVES[h]], bank[:], ACT.Sigmoid)

        turned_rows = (TILES - 1) * P
        rew_turned = {}
        for h in range(2):
            for d in range(D):
                bank = work_bank()
                c0 = 0
                for n in TURNED_WIDTHS:
                    nc.tensor.matmul_mx(
                        out=bank[:, c0 : c0 + n],
                        lhsT=dealt_w[h][:, d * P : (d + 1) * P].bitcast(FP8X4),
                        lhsT_scale=dealt_scales[:, h * HALF + d * P : h * HALF + (d + 1) * P],
                        rhs=w1_dw[:, 2 * (P + c0) : 2 * (P + c0 + n)].bitcast(FP4X4),
                        rhs_scale=w1_ds[:, P + c0 : P + c0 + n],
                        start=True,
                        stop=True,
                    )
                    c0 = c0 + n
                rew_turned[h, d] = keep.tile([P, turned_rows], F32, name="rew_turned%d%d" % (h, d))
                nc.scalar.activation(rew_turned[h, d][:], bank[:, 0:turned_rows], ACT.Sigmoid)

        base_gain = keep.tile([P, TILES], F32, name="base_gain")
        penalty_gain = keep.tile([P, TILES], F32, name="penalty_gain")
        nc.gpsimd.tensor_tensor(base_gain[:], inv_ref[:], unit_sb[:], ALU.mult)
        nc.gpsimd.tensor_scalar(penalty_gain[:], unit_sb[:], -PENALTY, 0.0, ALU.mult, ALU.add)

        pairs = keep.tile([P, 2, HALF // 2], F32, name="pairs")
        others0 = keep.tile([P, S], F32, name="others0")
        for h in range(2):
            two = rew0[:, HALVES[h]].rearrange("p (g e) -> p g e", e=2)
            nc.vector.tensor_tensor(pairs[:, h, :], two[:, :, 0], two[:, :, 1], ALU.add)
        for h in range(2):
            nc.vector.tensor_tensor(
                others0[:, HALVES[h]].rearrange("p (v g e) -> p v g e", g=2, e=2),
                rew0[:, HALVES[h]].rearrange("p (v g e) -> p v g e", g=2, e=2)[:, :, :, ::-1],
                pairs[:, h, :].rearrange("p (v g) -> p v g", g=2)[:, :, ::-1].unsqueeze(3).to_broadcast([P, HALF // D, 2, 2]),
                ALU.add,
            )

        adv = [keep.tile([P, S], F32, name="adv%d" % t) for t in range(TILES)]
        pgz = keep.tile([P, TILES, S], F32, name="pgz")
        hid = keep.tile([P, TILES, S], F32, name="hid")

        def by_member(ap):
            return ap.rearrange("p (d v) -> p v d", d=D)

        def by_group(ap):
            return ap.rearrange("p (v d) -> p v d", d=D)

        def turn(t, h):
            rows = slice((t - 1) * P, t * P)
            rest, own = work_bank(), work_bank()
            for d in range(D):
                mates = [e for e in range(D) if e != d]
                for e in mates:
                    nc.tensor.matmul(
                        rest[:, d * P : (d + 1) * P],
                        rew_turned[h, e][:, rows],
                        ident[:],
                        is_transpose=True,
                        start=(e == mates[0]),
                        stop=(e == mates[-1]),
                    )
            for d in range(D):
                nc.tensor.transpose(own[:, d * P : (d + 1) * P], rew_turned[h, d][:, rows], ident[:])
            return by_member(rest[:]), by_member(own[:])

        def advantage(t, sources):
            base = work.tile([P, S], F32, name="base")
            for h in range(2):
                nc.vector.scalar_tensor_tensor(
                    by_group(base[:, HALVES[h]]), sources[h][0], base_gain[:, t : t + 1], by_group(rel[t][:, HALVES[h]]),
                    ALU.mult, ALU.mult,
                )
            for h in range(2):
                nc.vector.scalar_tensor_tensor(
                    by_group(adv[t][:, HALVES[h]]), sources[h][1], unit_sb[:, t : t + 1], by_group(base[:, HALVES[h]]),
                    ALU.mult, ALU.subtract,
                )

        def log_prob(t, h):
            bank = psum.tile([P, HALF], F32, name="yl", bufs=8 - WORK_BANKS)
            row_product(bank, w2_dw, w2_ds, t, h)
            square = work.tile([P, HALF], F32, name="square", bufs=4)
            nc.scalar.activation(square[:], bank[:], ACT.Square)
            return bank, square

        def gradient_terms(t, yl):
            gated = [work.tile([P, HALF], F32, name="gated", bufs=3) for h in range(2)]
            for h in range(2):
                nc.vector.scalar_tensor_tensor(gated[h][:], yl[h][0][:], 0.0, adv[t][:, HALVES[h]], ALU.max, ALU.mult)
            for h in range(2):
                nc.vector.scalar_tensor_tensor(
                    pgz[:, t, HALVES[h]], yl[h][1][:], penalty_gain[:, t : t + 1], gated[h][:], ALU.mult, ALU.add
                )

        def fetch(t, c0, n):
            nc.vector.tensor_tensor(
                hid[:, t, c0 : c0 + n], adv[t][:].indirect(shuf_sb[:, c0 // 16 : (c0 + n) // 16]), pgz[:, t, c0 : c0 + n], ALU.add
            )

        def weave(c0, n):
            woven = keep.tile([P, n * TILES], BF16, name="woven%d" % c0, align_bytes=64)
            copy = nc.vector.tensor_copy if n == P else nc.scalar.copy
            copy(
                woven[:].rearrange("p (c i t) -> p c t i", i=4, t=TILES),
                hid[:, :, c0 : c0 + n].rearrange("p t (c i) -> p c t i", i=4),
            )
            return woven

        out_rows = out.rearrange("(a p) j -> p a j", p=P)

        def finish(c0, n, woven):
            codes = keep.tile([P, n], U32, name="codes%d" % c0, align_bytes=64)
            scales = keep.tile([P, n], U8, name="scales%d" % c0, align_bytes=64)
            nc.vector.quantize_mx(out=codes[:].bitcast(FP8X4), scales=scales[:], in_=woven[:])
            bank = work_bank()
            for a in range(N // P):
                nc.tensor.matmul_mx(
                    out=bank[:, a * n : (a + 1) * n],
                    lhsT=w3_w[:, 2 * P * a : 2 * P * (a + 1)].bitcast(FP4X4),
                    lhsT_scale=w3_s[:, P * a : P * (a + 1)],
                    rhs=codes[:].bitcast(FP8X4),
                    rhs_scale=scales[:],
                    start=True,
                    stop=True,
                )
            result = keep.tile([P, N // P, n], F32, name="result%d" % c0)
            empty = nc.vector.tensor_copy if c0 + n == S else nc.scalar.copy
            empty(result[:].rearrange("p a j -> p (a j)"), bank[:, 0 : N // P * n])
            nc.sync.dma_start(out=out_rows[:, :, c0 : c0 + n], in_=result[:])

        sources = [(by_group(others0[:, HALVES[h]]), by_group(rew0[:, HALVES[h]])) for h in range(2)]
        log_late = keep.tile([P, TILES - EARLY, S], F32, name="log_late", tag="w1_then_logs", align_bytes=64)
        for t in range(TILES):
            yl = [log_prob(t, h) for h in range(2)]
            for u in range(EARLY, TILES):
                if t == 0:
                    nc.scalar.activation(log_late[:, u - EARLY, :], den_sb[u][:], ACT.Ln, scale=inv_ref[:, u : u + 1])
                if t == 1:
                    nc.scalar.activation(rel[u], log_late[:, u - EARLY, :], ACT.Exp, scale=-1.0)
            advantage(t, sources)
            if t + 1 < TILES:
                sources = [turn(t + 1, h) for h in range(2)]
            gradient_terms(t, yl)
            if t < TILES - LATE_FETCH:
                for h in range(2):
                    fetch(t, h * HALF, HALF)

        waiting = None
        for c0, n in BLOCKS:
            for t in range(TILES - LATE_FETCH, TILES):
                fetch(t, c0, n)
            woven = weave(c0, n)
            if waiting is not None:
                finish(*waiting)
            waiting = (c0, n, woven)
        finish(*waiting)
